import numpy as np
import ml_dtypes


def mxq(x, axis, fmt="e4m3"):
    dtype, down = {"e4m3": (ml_dtypes.float8_e4m3fn, 7), "e5m2": (ml_dtypes.float8_e5m2, 14)}[fmt]
    v = np.moveaxis(np.asarray(x, np.float32).astype(ml_dtypes.bfloat16).astype(np.float64), axis, -1)
    blocks = v.reshape(v.shape[:-1] + (-1, 32))
    amax = np.abs(blocks).max(-1, keepdims=True)
    byte = np.maximum(np.where(amax > 0, np.frexp(amax)[1] - 1 + 127, 0) - down, 1)
    scale = np.exp2(byte - 127.0)
    codes = (blocks / scale).astype(np.float32).astype(dtype).astype(np.float64)
    return np.moveaxis((codes * scale).reshape(v.shape), -1, axis)


WIDE = False


def mx_kscale(k):
    if not WIDE:
        return np.ones(k)
    levels = np.array([10, -10, 5, -5, 0])
    if k % 512:
        return np.exp2(np.random.permutation(np.resize(levels, k // 32))).repeat(32)
    a = np.empty((k // 512, 16))
    for p in range(k // 512):
        a[p, :8] = np.random.permutation(np.resize(levels, 8))
        for g in range(8):
            far = levels[np.abs(levels - a[p, g]) >= 10]
            a[p, g + 8] = far[np.random.randint(len(far))]
    return np.exp2(a.ravel()).repeat(32)


BF16 = ml_dtypes.bfloat16


def bf(x):
    return np.asarray(x, np.float32).astype(BF16)


def f64(x):
    return np.asarray(x).astype(np.float64)


E2M1 = np.array([0.0, 0.5, 1.0, 1.5, 2.0, 3.0, 4.0, 6.0, -0.0, -0.5, -1.0, -1.5, -2.0, -3.0, -4.0, -6.0])


def pack_weight(w, fmt):
    k, n = w.shape
    w = f64(bf(w)).reshape(k // 32, 32, n)
    amax = np.abs(w).max(1)
    if fmt == "e4m3":
        byte = np.frexp(amax)[1] - 1 + 127 - 7
    else:
        mant, ex = np.frexp(amax / 6.0)
        byte = np.where(mant > 0.5, ex, ex - 1) + 127
    byte = np.clip(np.where(amax > 0, byte, 1), 1, 254)
    scaled = (w * np.exp2(127.0 - byte)[:, None, :]).reshape(k, n).astype(np.float32)
    by_word = np.ascontiguousarray(scaled.reshape(k // 512, 128, 4, n).transpose(0, 1, 3, 2))
    if fmt == "e4m3":
        words = by_word.astype(ml_dtypes.float8_e4m3fn).view(np.uint8)
    else:
        c = by_word.astype(ml_dtypes.float4_e2m1fn).view(np.uint8) & 0xF
        words = c[..., 0::2] | (c[..., 1::2] << 4)
    return np.ascontiguousarray(words), np.ascontiguousarray(byte.astype(np.uint8).reshape(k // 512, 16, n))


def unpack_weight(words, scales, fmt):
    g, p, n, _ = words.shape
    if fmt == "e4m3":
        vals = np.ascontiguousarray(words).view(ml_dtypes.float8_e4m3fn).astype(np.float64)
    else:
        nib = np.empty((g, p, n, 4), np.uint8)
        nib[..., 0::2] = words & 0xF
        nib[..., 1::2] = words >> 4
        vals = E2M1[nib]
    vals = vals * np.repeat(np.exp2(scales.astype(np.float64) - 127.0), 8, axis=1)[..., None]
    return vals.transpose(0, 1, 3, 2).reshape(g * 512, n)
def pack4(w):
    words, scales = pack_weight(w, "e2m1")
    return words.reshape(words.shape[0], 128, -1), scales


def unpack4(words, scales):
    return unpack_weight(words.reshape(words.shape[0], 128, -1, 2), scales, "e2m1")


def planes(Y):
    n, m = Y.shape
    b = f64(bf(Y)).reshape(n // 32, 32, m)
    amax = np.abs(b).max(1)
    byte = np.clip(np.where(amax > 0, np.frexp(amax)[1] - 1 + 127 - 7, 1), 1, 254)
    codes = (b * np.exp2(127.0 - byte)[:, None, :]).reshape(n, m).astype(np.float32).astype(ml_dtypes.float8_e4m3fn).view(np.uint8)
    words = codes.reshape(n // 512, 128, 4, m).transpose(0, 1, 3, 2)
    return np.ascontiguousarray(words), np.ascontiguousarray(byte.astype(np.uint8).reshape(n // 512, 16, m))


R, A, H = 2048, 1024, 512

TAU = 2.0 * np.pi

def setup_inputs():
    s = mx_kscale(A)
    t = mx_kscale(H)
    theta = TAU * (np.arange(A) + 0.25 * np.random.rand(A)) / A
    order = np.arange(1, H // 2 + 1)
    phase = theta[:, None] * order[None, :]
    E = np.concatenate([np.cos(phase), np.sin(phase)], axis=1) * np.sqrt(2.0 / A)
    speed = 0.3 + 0.2 * np.random.rand(R, 1)
    heading = TAU * np.random.rand(R, 1)
    V = speed * np.cos(theta[None, :] - heading) + np.random.randn(R, A)
    gain = np.exp(0.8 * np.random.randn(A))
    vel_words, vel_scales = pack4(V.T * s[:, None])
    har_words, har_scales = pack4(E / s[:, None])
    return {
        "vel_words": vel_words, "vel_scales": vel_scales,
        "har_words": har_words, "har_scales": har_scales,
        "taper": bf(np.exp(-0.5 * np.random.rand(H)) * t),
        "background": bf(0.3 * np.random.randn(H) * t),
        "refit": bf(E.T * gain[None, :] / t[:, None]),
        "velocity": bf(V * gain[None, :]),
        "distance": bf(0.8 * np.random.randn(R, A)),
    }

def reference(vel_words, vel_scales, har_words, har_scales, taper, background, refit, velocity, distance):
    V = unpack4(vel_words, vel_scales)
    P = unpack4(har_words, har_scales)
    C = V.T @ P
    C = C * f64(taper) + f64(background)
    fit = mxq(C, 1, "e4m3") @ mxq(f64(refit), 0, "e4m3")
    y = (f64(velocity) - fit) * np.exp(-np.square(f64(distance)))
    words, scales = planes(y.T)
    return y, words, scales

@@ -1,0 +1,417 @@
+from contextlib import ExitStack
+
+import concourse.mybir as mybir
+from concourse.masks import make_identity
+
+R, A, H = 2048, 1024, 512
+FLOPS = 2 * R * A * H * 2
+
+F32 = mybir.dt.float32
+BF16 = mybir.dt.bfloat16
+I32 = mybir.dt.int32
+U32 = mybir.dt.uint32
+U8 = mybir.dt.uint8
+FP8X4 = mybir.dt.float8_e4m3fn_x4
+FP4X4 = mybir.dt.float4_e2m1fn_x4
+ACT = mybir.ActivationFunctionType
+ALU = mybir.AluOpType
+
+P = 128
+TILES = R // P
+GROUPS = A // 512
+CHUNKS = [(0, 1), (1, 1), (2, 2), (4, 4), (8, 4), (12, 4)]
+PLANE_SETS = [(0, 4), (4, 4), (8, 4), (12, 2), (14, 1), (15, 1)]
+WORD_LOADS = [(0, 2), (2, 6), (8, 8)]
+ROW_LOADS = [(0, 1), (1, 1), (2, 2), (4, 2), (6, 2), (8, 2), (10, 2), (12, 2), (14, 2)]
+
+
+SC_EARLY, SC_MID, SC_LATE = 16, 40, 64
+G_WORDS = 0
+HEAD_S = 0
+
+
+def scalar_cast_words(j):
+    if j < 9:
+        return SC_EARLY
+    if j < 14:
+        return SC_MID
+    return SC_LATE
+
+
+def tile_radar_azimuth_harmonic_residuals_k5_kernel(
+    tc, vel_words, vel_scales, har_words, har_scales, taper, background, refit, velocity, distance, out_0, out_1, out_2
+):
+    nc = tc.nc
+    with ExitStack() as ctx:
+        keep = ctx.enter_context(tc.tile_pool(name="keep", bufs=1))
+        flow = ctx.enter_context(tc.tile_pool(name="flow", bufs=2))
+        psum = ctx.enter_context(tc.psum_pool(name="psum", bufs=2))
+        ctx.enter_context(tc.manual_schedule())
+
+        ident = keep.tile([P, P], F32, name="ident")
+        har_raw = keep.tile([P, GROUPS, 2 * H], U8, name="har_raw", align_bytes=64)
+        har_sc_raw = keep.tile([P, GROUPS, H], U8, name="har_sc_raw", align_bytes=64)
+        har_codes = keep.tile([P, GROUPS, 4, 2 * P], U8, name="har_codes", align_bytes=64)
+        har_sc = keep.tile([P, GROUPS, 4, P], U8, name="har_sc", align_bytes=64)
+        vel_sc = keep.tile([P, GROUPS, R], U8, name="vel_sc", align_bytes=64)
+        taper_bf = keep.tile([P, 4], BF16, name="taper_bf")
+        back_bf = keep.tile([P, 4], BF16, name="back_bf")
+        taper_f = keep.tile([P, 4], F32, name="taper_f")
+        back_f = keep.tile([P, 4], F32, name="back_f")
+        warm = keep.tile([P, 1], F32, name="warm")
+        y_sc = keep.tile([P, GROUPS, R], U8, name="y_sc", align_bytes=64)
+
+        vel_codes = {}
+        vel_rows = {}
+        dist_rows = {}
+        refit_raw = {}
+        refit_grp = {}
+        refit_q = {}
+        c_bank = {}
+        c_slots = {}
+        c_grp = {}
+        c_q = {}
+        fit = {}
+        weight = {}
+        y = {}
+        y_bf = {}
+        xt = {}
+        q_in = {}
+        y_codes = {}
+
+        def owner(table, j):
+            return [entry for entry in table if entry[0] <= j < entry[0] + entry[1]][0]
+
+        def load_scale_rows(plane, rows):
+            for q in range(4):
+                nc.sync.dma_start(
+                    out=plane[32 * q : 32 * q + 4, :, :].bitcast(I32),
+                    in_=rows.rearrange("g q n -> q g n")[4 * q : 4 * q + 4, :, :].bitcast(I32),
+                )
+
+        def load_words(first, count):
+            t = keep.tile([P, GROUPS, 2 * P * count], U8, name="vel_codes%d" % first, align_bytes=64)
+            nc.sync.dma_start(
+                out=t[:].bitcast(I32),
+                in_=vel_words.rearrange("g p n -> p g n")[:, :, 2 * P * first : 2 * P * (first + count)].bitcast(I32),
+            )
+            vel_codes[first] = t
+
+        def load_rows(store, src, label, first, count):
+            t = keep.tile([P, count, A], BF16, name="%s%d" % (label, first))
+            nc.sync.dma_start(
+                out=t[:], in_=src[P * first : P * (first + count), :].rearrange("(j p) a -> p j a", p=P)
+            )
+            for j in range(count):
+                store[first + j] = t[:, j, :]
+
+        def load_refit(g):
+            t = keep.tile([P, 4, 512], BF16, name="refit_raw%d" % g)
+            nc.sync.dma_start(out=t[:], in_=refit[:, 512 * g : 512 * (g + 1)].rearrange("(p t) a -> p t a", t=4))
+            refit_raw[g] = t
+
+        def group_refit(g, on_scalar):
+            t = keep.tile([P, 512, 4], BF16, name="refit_grp%d" % g, align_bytes=64)
+            src = refit_raw[g][:].rearrange("p t a -> p a t")
+            if on_scalar:
+                nc.scalar.copy(out=t[:], in_=src)
+            else:
+                nc.vector.tensor_copy(out=t[:], in_=src)
+            refit_grp[g] = t
+
+        def quantize_refit(g):
+            codes = keep.tile([P, 512], U32, name="refit_codes%d" % g, align_bytes=64)
+            scales = keep.tile([P, 512], U8, name="refit_sc%d" % g, align_bytes=64)
+            nc.vector.quantize_mx(
+                out=codes[:].bitcast(FP8X4), scales=scales[:], in_=refit_grp[g][:].rearrange("p a t -> p (a t)")
+            )
+            refit_q[g] = (codes, scales)
+
+        def project(first, count, t):
+            n = P * count
+            per_bank = 4 // count
+            if t % per_bank == 0:
+                bank = psum.tile([P, 512], F32, name="c_bank", tag="c_bank", bufs=2)
+                c_bank[first, t // per_bank] = bank
+            dst = c_bank[first, t // per_bank][:, n * (t % per_bank) : n * (t % per_bank + 1)]
+            w_first, w_count = owner(WORD_LOADS, first)
+            off = P * (first - w_first)
+            for g in range(GROUPS):
+                nc.tensor.matmul_mx(
+                    out=dst,
+                    lhsT=har_codes[:, g, t, :].bitcast(FP4X4),
+                    lhsT_scale=har_sc[:, g, t, :],
+                    rhs=vel_codes[w_first][:, g, 2 * off : 2 * (off + n)].bitcast(FP4X4),
+                    rhs_scale=vel_sc[:, g, P * first : P * first + n],
+                    start=(g == 0),
+                    stop=(g == GROUPS - 1),
+                )
+
+        def taper_slot(first, count, t):
+            n = P * count
+            per_bank = 4 // count
+            if t == 0:
+                slots = flow.tile([P, 4, n], BF16, name="c_slots", tag="c_slots", bufs=2)
+                c_slots[first] = slots
+            src = c_bank[first, t // per_bank][:, n * (t % per_bank) : n * (t % per_bank + 1)]
+            nc.scalar.activation(
+                out=c_slots[first][:, t, :],
+                in_=src,
+                func=ACT.Identity,
+                scale=taper_f[:, t : t + 1],
+                bias=back_f[:, t : t + 1],
+            )
+
+        def group_c(first, count):
+            n = P * count
+            t = flow.tile([P, n, 4], BF16, name="c_grp", tag="c_grp", bufs=2, align_bytes=64)
+            nc.vector.tensor_copy(out=t[:], in_=c_slots[first][:].rearrange("p t r -> p r t"))
+            c_grp[first] = t
+
+        def quantize_c(first, count):
+            n = P * count
+            codes = keep.tile([P, n], U32, name="c_codes%d" % first, align_bytes=64)
+            scales = keep.tile([P, n], U8, name="c_sc%d" % first, align_bytes=64)
+            nc.vector.quantize_mx(
+                out=codes[:].bitcast(FP8X4), scales=scales[:], in_=c_grp[first][:].rearrange("p r t -> p (r t)")
+            )
+            c_q[first] = (codes, scales)
+
+        def refit_rings(j, g):
+            first, count = owner(CHUNKS, j)
+            codes, scales = c_q[first]
+            cols = slice(P * (j - first), P * (j - first + 1))
+            bank = psum.tile([P, 512], F32, name="fit", tag="fit", bufs=4)
+            nc.tensor.matmul_mx(
+                out=bank[:],
+                lhsT=codes[:, cols].bitcast(FP8X4),
+                lhsT_scale=scales[:, cols],
+                rhs=refit_q[g][0][:].bitcast(FP8X4),
+                rhs_scale=refit_q[g][1][:],
+                start=True,
+                stop=True,
+            )
+            fit[j, g] = bank
+
+        def square(j):
+            t = flow.tile([P, A], F32, name="weight", tag="weight", bufs=4)
+            nc.scalar.activation(out=t[:], in_=dist_rows[j], func=ACT.Square)
+            weight[j] = t
+
+        def gaussian(j):
+            nc.scalar.activation(out=weight[j][:], in_=weight[j][:], func=ACT.Exp, scale=-1.0)
+
+        def subtract(j, g):
+            if g == 0:
+                t = flow.tile([P, A], F32, name="y", tag="y", bufs=7)
+                y[j] = t
+            cols = slice(512 * g, 512 * (g + 1))
+            nc.vector.tensor_tensor(out=y[j][:, cols], in0=vel_rows[j][:, cols], in1=fit[j, g][:], op=ALU.subtract)
+
+        def weigh(j, halves=(0, 1)):
+            cols = slice(512 * halves[0], 512 * (halves[-1] + 1))
+            nc.vector.tensor_tensor(out=y[j][:, cols], in0=y[j][:, cols], in1=weight[j][:, cols], op=ALU.mult)
+            nc.sync.dma_start(out=out_0[P * j : P * (j + 1), cols], in_=y[j][:, cols])
+
+        def round_views(j):
+            if j not in y_bf:
+                t = flow.tile([P, A], BF16, name="y_bf", tag="y_bf", bufs=3, align_bytes=64)
+                y_bf[j] = t
+            dst = y_bf[j][:].rearrange("p (u g m e) -> p u g m e", g=GROUPS, u=2, e=2)
+            src = y[j][:].rearrange("p (g m u e) -> p u g m e", g=GROUPS, u=2, e=2)
+            return dst, src
+
+        def round_vector(j):
+            lo, hi = G_WORDS, P - scalar_cast_words(j)
+            if hi > lo:
+                dst, src = round_views(j)
+                nc.vector.tensor_copy(out=dst[:, :, :, lo:hi, :], in_=src[:, :, :, lo:hi, :])
+
+        def round_scalar(j):
+            lo = max(G_WORDS, P - scalar_cast_words(j))
+            if lo < P:
+                dst, src = round_views(j)
+                nc.scalar.copy(out=dst[:, :, :, lo:, :], in_=src[:, :, :, lo:, :])
+
+        def round_gpsimd(j):
+            if G_WORDS > 0:
+                dst, src = round_views(j)
+                assert G_WORDS == P
+                nc.gpsimd.tensor_scalar(
+                    out=dst.rearrange("p u g m e -> p u (g m) e"), in0=src.rearrange("p u g m e -> p u (g m) e"),
+                    scalar1=1.0, scalar2=1.0, op0=ALU.mult, op1=ALU.mult,
+                )
+
+        def round_half(j, g):
+            dst, src = round_views(j)
+            nc.vector.tensor_copy(out=dst[:, :, g], in_=src[:, :, g])
+
+        def turn(j, halves=(0, 1)):
+            bank = psum.tile([P, 4, P], F32, name="xt", tag="xt", bufs=2)
+            words = y_bf[j][:].bitcast(F32)
+            for g in halves:
+                for u in range(2):
+                    i = GROUPS * u + g
+                    nc.tensor.transpose(bank[:, 2 * g + u, :], words[:, P * i : P * (i + 1)], ident[:])
+                xt[j, g] = bank
+
+        def gather(j, halves=(0, 1)):
+            first, count = owner(PLANE_SETS, j)
+            if first not in q_in:
+                t = flow.tile([P, GROUPS, 4 * P * count], BF16, name="q_in", tag="q_in", bufs=3, align_bytes=64)
+                q_in[first] = t
+            gs = slice(halves[0], halves[-1] + 1)
+            words = q_in[first][:].bitcast(F32)[:, gs, 2 * P * (j - first) : 2 * P * (j - first + 1)]
+            nc.scalar.copy(
+                out=words.rearrange("p g (r u) -> p g r u", u=2),
+                in_=xt[j, halves[0]][:].rearrange("p (g u) r -> p g r u", u=2)[:, gs],
+            )
+
+        def quantize_y(first, count, g):
+            n = P * count
+            if g == 0:
+                t = flow.tile([P, GROUPS, n], U32, name="y_codes", tag="y_codes", bufs=3, align_bytes=64)
+                y_codes[first] = t
+            nc.vector.quantize_mx(
+                out=y_codes[first][:, g, :].bitcast(FP8X4),
+                scales=y_sc[:, g, P * first : P * first + n],
+                in_=q_in[first][:, g, :],
+            )
+            if g == GROUPS - 1:
+                dst = out_1.rearrange("g p m t -> p g (m t)")[:, :, 4 * P * first : 4 * (P * first + n)]
+                nc.sync.dma_start(out=dst.bitcast(I32), in_=y_codes[first][:].bitcast(I32))
+
+        nc.vector.memset(har_sc_raw[:].rearrange("p g n -> p (g n)").bitcast(I32), 0)
+        nc.vector.memset(vel_sc[:].rearrange("p g n -> p (g n)").bitcast(I32), 0)
+        nc.vector.memset(warm[:], 0.0)
+        nc.gpsimd.dma_start(out=taper_bf[:], in_=taper.rearrange("(p t) -> p t", t=4))
+        nc.gpsimd.dma_start(out=back_bf[:], in_=background.rearrange("(p t) -> p t", t=4))
+        make_identity(nc, ident[:])
+        nc.scalar.activation(out=warm[:], in_=warm[:], func=ACT.Exp)
+
+        nc.sync.dma_start(out=har_raw[:].bitcast(I32), in_=har_words.rearrange("g p n -> p g n").bitcast(I32))
+        load_scale_rows(har_sc_raw, har_scales)
+        load_rows(dist_rows, distance, "dist", *ROW_LOADS[0])
+        load_words(*WORD_LOADS[0])
+        load_refit(HEAD_S)
+        load_scale_rows(vel_sc, vel_scales)
+        load_refit(1 - HEAD_S)
+        load_words(*WORD_LOADS[1])
+        load_rows(dist_rows, distance, "dist", *ROW_LOADS[1])
+        load_rows(vel_rows, velocity, "vel", *ROW_LOADS[0])
+        load_rows(vel_rows, velocity, "vel", *ROW_LOADS[1])
+        for i, entry in enumerate(ROW_LOADS[2:]):
+            load_rows(dist_rows, distance, "dist", *entry)
+            load_rows(vel_rows, velocity, "vel", *entry)
+            if i == 0:
+                load_words(*WORD_LOADS[2])
+
+        nc.gpsimd.tensor_copy(out=taper_f[:], in_=taper_bf[:])
+        nc.gpsimd.tensor_copy(out=back_f[:], in_=back_bf[:])
+
+        nc.vector.tensor_copy(out=har_sc[:], in_=har_sc_raw[:].rearrange("p g (m t) -> p g t m", t=4))
+        har_view = har_raw[:].rearrange("p g (m t b) -> p g t m b", t=4, b=2)
+        for t in range(4):
+            nc.vector.tensor_copy(
+                out=har_codes[:, :, t, :].rearrange("p g (m b) -> p g m b", b=2), in_=har_view[:, :, t, :, :]
+            )
+        square(0)
+        gaussian(0)
+        for t in range(4):
+            project(*CHUNKS[0], t)
+        for t in range(4):
+            project(*CHUNKS[1], t)
+        if HEAD_S:
+            group_refit(1, True)
+        group_refit(0, False)
+        for t in range(4):
+            taper_slot(*CHUNKS[0], t)
+        for t in range(4):
+            taper_slot(*CHUNKS[1], t)
+        for t in range(4):
+            project(*CHUNKS[2], t)
+        quantize_refit(0)
+        if not HEAD_S:
+            group_refit(1, False)
+        group_c(*CHUNKS[0])
+        quantize_refit(1)
+        quantize_c(*CHUNKS[0])
+        group_c(*CHUNKS[1])
+        for g in range(GROUPS):
+            refit_rings(0, g)
+        for t in range(4):
+            taper_slot(*CHUNKS[2], t)
+        quantize_c(*CHUNKS[1])
+        for t in range(2):
+            project(*CHUNKS[3], t)
+        for g in range(GROUPS):
+            refit_rings(1, g)
+        subtract(0, 0)
+        group_c(*CHUNKS[2])
+        subtract(0, 1)
+        quantize_c(*CHUNKS[2])
+        for t in range(2):
+            taper_slot(*CHUNKS[3], t)
+        for t in range(2, 4):
+            project(*CHUNKS[3], t)
+
+        extras = {}
+        for first, count in CHUNKS[3:]:
+            extras.setdefault(first - 4 + (first == 4), []).append((group_c, (first, count)))
+            extras.setdefault(first - 3, []).append((quantize_c, (first, count)))
+        for first, count in PLANE_SETS[:-1]:
+            ready = first + count + (2 if first < 8 else 1)
+            for g in range(GROUPS):
+                at = ready + g if count == 4 else ready
+                extras.setdefault(at, []).append((quantize_y, (first, count, g)))
+
+        last = TILES - 1
+        for s in range(last):
+            if s + 8 < TILES and s > 0:
+                project(8 + 4 * (s // 4), 4, s % 4)
+            if s + 2 < TILES:
+                for g in range(GROUPS):
+                    refit_rings(s + 2, g)
+            if s >= 1:
+                turn(s - 1)
+            square(s + 1)
+            subtract(s + 1, 0)
+            weigh(s)
+            round_gpsimd(s)
+            if s == 0:
+                taper_slot(*CHUNKS[3], 2)
+                project(8, 4, 0)
+            if s >= 2:
+                gather(s - 2)
+            gaussian(s + 1)
+            subtract(s + 1, 1)
+            round_vector(s)
+            if s == 0:
+                taper_slot(*CHUNKS[3], 3)
+            if s + 8 < TILES:
+                taper_slot(8 + 4 * (s // 4), 4, s % 4)
+            round_scalar(s)
+            for fn, args in extras.get(s, []):
+                fn(*args)
+
+        turn(last - 1)
+        gather(last - 2)
+        weigh(last, (0,))
+        gather(last - 1)
+        weigh(last, (1,))
+        round_half(last, 0)
+        turn(last, (0,))
+        round_half(last, 1)
+        turn(last, (1,))
+        for s in (last, last + 1):
+            for fn, args in extras.get(s, []):
+                fn(*args)
+        for g in range(GROUPS):
+            gather(last, (g,))
+            quantize_y(last, 1, g)
+
+        for q in range(4):
+            nc.sync.dma_start(
+                out=out_2.rearrange("g q m -> q g m")[4 * q : 4 * q + 4, :, :].bitcast(I32),
+                in_=y_sc[32 * q : 32 * q + 4, :, :].bitcast(I32),
+            )

@@ -20,22 +20,14 @@ P = 128
 TILES = R // P
 GROUPS = A // 512
 CHUNKS = [(0, 1), (1, 1), (2, 2), (4, 4), (8, 4), (12, 4)]
-PLANE_SETS = [(0, 4), (4, 4), (8, 4), (12, 2), (14, 1), (15, 1)]
+UNITS = [(0, 1), (1, 1), (2, 2), (4, 2), (6, 2), (8, 2), (10, 2), (12, 2), (14, 2)]
+PLANE_SETS = [(0, 4), (4, 4), (8, 2), (10, 2), (12, 2), (14, 2)]
 WORD_LOADS = [(0, 2), (2, 6), (8, 8)]
-ROW_LOADS = [(0, 1), (1, 1), (2, 2), (4, 2), (6, 2), (8, 2), (10, 2), (12, 2), (14, 2)]
-
-
-SC_EARLY, SC_MID, SC_LATE = 16, 40, 64
-G_WORDS = 0
-HEAD_S = 0
-
-
-def scalar_cast_words(j):
-    if j < 9:
-        return SC_EARLY
-    if j < 14:
-        return SC_MID
-    return SC_LATE
+G_SHARE = 224
+S_CAST = ()
+V_GATHER = ()
+AHEAD = 4
+LEAD = 1
 
 
 def tile_radar_azimuth_harmonic_residuals_k5_kernel(
@@ -57,7 +49,6 @@ def tile_radar_azimuth_harmonic_residuals_k5_kernel(
         taper_bf = keep.tile([P, 4], BF16, name="taper_bf")
         back_bf = keep.tile([P, 4], BF16, name="back_bf")
         taper_f = keep.tile([P, 4], F32, name="taper_f")
-        back_f = keep.tile([P, 4], F32, name="back_f")
         warm = keep.tile([P, 1], F32, name="warm")
         y_sc = keep.tile([P, GROUPS, R], U8, name="y_sc", align_bytes=64)
 
@@ -97,26 +88,27 @@ def tile_radar_azimuth_harmonic_residuals_k5_kernel(
             )
             vel_codes[first] = t
 
-        def load_rows(store, src, label, first, count):
-            t = keep.tile([P, count, A], BF16, name="%s%d" % (label, first))
+        def load_rows(store, src, label, k):
+            first, count = UNITS[k]
+            t = flow.tile([P, count, A], BF16, name=label, tag=label, bufs=AHEAD + 1)
             nc.sync.dma_start(
                 out=t[:], in_=src[P * first : P * (first + count), :].rearrange("(j p) a -> p j a", p=P)
             )
-            for j in range(count):
-                store[first + j] = t[:, j, :]
+            store[k] = t
 
         def load_refit(g):
             t = keep.tile([P, 4, 512], BF16, name="refit_raw%d" % g)
             nc.sync.dma_start(out=t[:], in_=refit[:, 512 * g : 512 * (g + 1)].rearrange("(p t) a -> p t a", t=4))
             refit_raw[g] = t
 
-        def group_refit(g, on_scalar):
+        def interleave(dst, src):
+            nc.vector.tensor_copy(
+                out=dst.rearrange("p (c i) t -> p c t i", i=4), in_=src.rearrange("p t (c i) -> p c t i", i=4)
+            )
+
+        def group_refit(g):
             t = keep.tile([P, 512, 4], BF16, name="refit_grp%d" % g, align_bytes=64)
-            src = refit_raw[g][:].rearrange("p t a -> p a t")
-            if on_scalar:
-                nc.scalar.copy(out=t[:], in_=src)
-            else:
-                nc.vector.tensor_copy(out=t[:], in_=src)
+            interleave(t[:], refit_raw[g][:])
             refit_grp[g] = t
 
         def quantize_refit(g):
@@ -159,13 +151,13 @@ def tile_radar_azimuth_harmonic_residuals_k5_kernel(
                 in_=src,
                 func=ACT.Identity,
                 scale=taper_f[:, t : t + 1],
-                bias=back_f[:, t : t + 1],
+                bias=back_bf[:, t : t + 1],
             )
 
         def group_c(first, count):
             n = P * count
             t = flow.tile([P, n, 4], BF16, name="c_grp", tag="c_grp", bufs=2, align_bytes=64)
-            nc.vector.tensor_copy(out=t[:], in_=c_slots[first][:].rearrange("p t r -> p r t"))
+            interleave(t[:], c_slots[first][:])
             c_grp[first] = t
 
         def quantize_c(first, count):
@@ -177,95 +169,106 @@ def tile_radar_azimuth_harmonic_residuals_k5_kernel(
             )
             c_q[first] = (codes, scales)
 
-        def refit_rings(j, g):
-            first, count = owner(CHUNKS, j)
-            codes, scales = c_q[first]
-            cols = slice(P * (j - first), P * (j - first + 1))
-            bank = psum.tile([P, 512], F32, name="fit", tag="fit", bufs=4)
-            nc.tensor.matmul_mx(
-                out=bank[:],
-                lhsT=codes[:, cols].bitcast(FP8X4),
-                lhsT_scale=scales[:, cols],
-                rhs=refit_q[g][0][:].bitcast(FP8X4),
-                rhs_scale=refit_q[g][1][:],
-                start=True,
-                stop=True,
-            )
-            fit[j, g] = bank
+        def refit_rings(k):
+            unit_first, unit_count = UNITS[k]
+            for j in range(unit_first, unit_first + unit_count):
+                first, count = owner(CHUNKS, j)
+                codes, scales = c_q[first]
+                cols = slice(P * (j - first), P * (j - first + 1))
+                for g in reversed(range(GROUPS)):
+                    bank = psum.tile([P, 512], F32, name="fit", tag="fit", bufs=4)
+                    nc.tensor.matmul_mx(
+                        out=bank[:],
+                        lhsT=codes[:, cols].bitcast(FP8X4),
+                        lhsT_scale=scales[:, cols],
+                        rhs=refit_q[g][0][:].bitcast(FP8X4),
+                        rhs_scale=refit_q[g][1][:],
+                        start=True,
+                        stop=True,
+                    )
+                    fit[j, g] = bank
 
-        def square(j):
-            t = flow.tile([P, A], F32, name="weight", tag="weight", bufs=4)
-            nc.scalar.activation(out=t[:], in_=dist_rows[j], func=ACT.Square)
-            weight[j] = t
+        def square(k):
+            t = flow.tile([P, UNITS[k][1], A], F32, name="weight", tag="weight", bufs=3)
+            nc.scalar.activation(out=t[:], in_=dist_rows[k][:], func=ACT.Square)
+            weight[k] = t
 
-        def gaussian(j):
-            nc.scalar.activation(out=weight[j][:], in_=weight[j][:], func=ACT.Exp, scale=-1.0)
+        def gaussian(k):
+            nc.scalar.activation(out=weight[k][:], in_=weight[k][:], func=ACT.Exp, scale=-1.0)
 
-        def subtract(j, g):
-            if g == 0:
-                t = flow.tile([P, A], F32, name="y", tag="y", bufs=7)
-                y[j] = t
-            cols = slice(512 * g, 512 * (g + 1))
-            nc.vector.tensor_tensor(out=y[j][:, cols], in0=vel_rows[j][:, cols], in1=fit[j, g][:], op=ALU.subtract)
+        def subtract(k):
+            first, count = UNITS[k]
+            t = flow.tile([P, count, A], F32, name="y", tag="y", bufs=4)
+            y[k] = t
+            for j in range(count):
+                for g in range(GROUPS):
+                    cols = slice(512 * g, 512 * (g + 1))
+                    nc.vector.tensor_tensor(
+                        out=t[:, j, cols], in0=vel_rows[k][:, j, cols], in1=fit[first + j, g][:], op=ALU.subtract
+                    )
 
-        def weigh(j, halves=(0, 1)):
-            cols = slice(512 * halves[0], 512 * (halves[-1] + 1))
-            nc.vector.tensor_tensor(out=y[j][:, cols], in0=y[j][:, cols], in1=weight[j][:, cols], op=ALU.mult)
-            nc.sync.dma_start(out=out_0[P * j : P * (j + 1), cols], in_=y[j][:, cols])
+        def weigh(k, tiles=slice(None), cols=slice(None)):
+            first, count = UNITS[k]
+            part = y[k][:, tiles, cols]
+            nc.vector.tensor_tensor(out=part, in0=part, in1=weight[k][:, tiles, cols], op=ALU.mult)
+            dst = out_0[P * first : P * (first + count), :].rearrange("(j p) a -> p j a", p=P)
+            nc.sync.dma_start(out=dst[:, tiles, cols], in_=part)
 
-        def round_views(j):
-            if j not in y_bf:
-                t = flow.tile([P, A], BF16, name="y_bf", tag="y_bf", bufs=3, align_bytes=64)
-                y_bf[j] = t
-            dst = y_bf[j][:].rearrange("p (u g m e) -> p u g m e", g=GROUPS, u=2, e=2)
-            src = y[j][:].rearrange("p (g m u e) -> p u g m e", g=GROUPS, u=2, e=2)
-            return dst, src
+        def round_views(k):
+            count = UNITS[k][1]
+            if k not in y_bf:
+                t = flow.tile([P, 2, 2 * P * count, 2], BF16, name="y_bf", tag="y_bf", bufs=2, align_bytes=64)
+                y_bf[k] = t
+            return y_bf[k][:], y[k][:].rearrange("p j (w u e) -> p u (j w) e", u=2, e=2)
 
-        def round_vector(j):
-            lo, hi = G_WORDS, P - scalar_cast_words(j)
-            if hi > lo:
-                dst, src = round_views(j)
-                nc.vector.tensor_copy(out=dst[:, :, :, lo:hi, :], in_=src[:, :, :, lo:hi, :])
+        def split(k):
+            return (G_SHARE if k in S_CAST else 2 * P) * UNITS[k][1]
 
-        def round_scalar(j):
-            lo = max(G_WORDS, P - scalar_cast_words(j))
-            if lo < P:
-                dst, src = round_views(j)
-                nc.scalar.copy(out=dst[:, :, :, lo:, :], in_=src[:, :, :, lo:, :])
-
-        def round_gpsimd(j):
-            if G_WORDS > 0:
-                dst, src = round_views(j)
-                assert G_WORDS == P
+        def round_gpsimd(k):
+            if split(k) > 0:
+                dst, src = round_views(k)
                 nc.gpsimd.tensor_scalar(
-                    out=dst.rearrange("p u g m e -> p u (g m) e"), in0=src.rearrange("p u g m e -> p u (g m) e"),
+                    out=dst[:, :, : split(k), :], in0=src[:, :, : split(k), :],
                     scalar1=1.0, scalar2=1.0, op0=ALU.mult, op1=ALU.mult,
                 )
 
-        def round_half(j, g):
-            dst, src = round_views(j)
-            nc.vector.tensor_copy(out=dst[:, :, g], in_=src[:, :, g])
+        def round_rest(k, on_scalar):
+            if split(k) < 2 * P * UNITS[k][1] and on_scalar == (k in S_CAST):
+                dst, src = round_views(k)
+                if on_scalar:
+                    nc.scalar.copy(out=dst[:, :, split(k) :, :], in_=src[:, :, split(k) :, :])
+                else:
+                    nc.vector.tensor_copy(out=dst[:, :, split(k) :, :], in_=src[:, :, split(k) :, :])
 
-        def turn(j, halves=(0, 1)):
-            bank = psum.tile([P, 4, P], F32, name="xt", tag="xt", bufs=2)
-            words = y_bf[j][:].bitcast(F32)
+        def round_part(k, lo, hi, on_scalar):
+            dst, src = round_views(k)
+            if on_scalar:
+                nc.scalar.copy(out=dst[:, :, lo:hi, :], in_=src[:, :, lo:hi, :])
+            else:
+                nc.vector.tensor_copy(out=dst[:, :, lo:hi, :], in_=src[:, :, lo:hi, :])
+
+        def turn(k, j, halves=(0, 1), tag="xt", bufs=2):
+            words = y_bf[k][:].rearrange("p u w e -> p u (w e)").bitcast(F32)
+            bank = psum.tile([P, 4, P], F32, name="xt", tag=tag, bufs=bufs)
             for g in halves:
                 for u in range(2):
-                    i = GROUPS * u + g
-                    nc.tensor.transpose(bank[:, 2 * g + u, :], words[:, P * i : P * (i + 1)], ident[:])
-                xt[j, g] = bank
+                    off = P * (GROUPS * j + g)
+                    nc.tensor.transpose(bank[:, 2 * g + u, :], words[:, u, off : off + P], ident[:])
+                xt[UNITS[k][0] + j, g] = bank
 
-        def gather(j, halves=(0, 1)):
+        def gather(j, on_scalar, halves=(0, 1)):
             first, count = owner(PLANE_SETS, j)
             if first not in q_in:
-                t = flow.tile([P, GROUPS, 4 * P * count], BF16, name="q_in", tag="q_in", bufs=3, align_bytes=64)
+                t = flow.tile([P, GROUPS, 4 * P * count], BF16, name="q_in", tag="q_in", bufs=4, align_bytes=64)
                 q_in[first] = t
             gs = slice(halves[0], halves[-1] + 1)
             words = q_in[first][:].bitcast(F32)[:, gs, 2 * P * (j - first) : 2 * P * (j - first + 1)]
-            nc.scalar.copy(
-                out=words.rearrange("p g (r u) -> p g r u", u=2),
-                in_=xt[j, halves[0]][:].rearrange("p (g u) r -> p g r u", u=2)[:, gs],
-            )
+            dst = words.rearrange("p g (r u) -> p g r u", u=2)
+            src = xt[j, halves[0]][:].rearrange("p (g u) r -> p g r u", u=2)[:, gs]
+            if on_scalar:
+                nc.scalar.copy(out=dst, in_=src)
+            else:
+                nc.vector.tensor_copy(out=dst, in_=src)
 
         def quantize_y(first, count, g):
             n = P * count
@@ -291,23 +294,21 @@ def tile_radar_azimuth_harmonic_residuals_k5_kernel(
 
         nc.sync.dma_start(out=har_raw[:].bitcast(I32), in_=har_words.rearrange("g p n -> p g n").bitcast(I32))
         load_scale_rows(har_sc_raw, har_scales)
-        load_rows(dist_rows, distance, "dist", *ROW_LOADS[0])
+        load_rows(dist_rows, distance, "dist", 0)
         load_words(*WORD_LOADS[0])
-        load_refit(HEAD_S)
+        load_refit(0)
         load_scale_rows(vel_sc, vel_scales)
-        load_refit(1 - HEAD_S)
+        load_rows(dist_rows, distance, "dist", 1)
+        load_refit(1)
+        load_rows(dist_rows, distance, "dist", 2)
         load_words(*WORD_LOADS[1])
-        load_rows(dist_rows, distance, "dist", *ROW_LOADS[1])
-        load_rows(vel_rows, velocity, "vel", *ROW_LOADS[0])
-        load_rows(vel_rows, velocity, "vel", *ROW_LOADS[1])
-        for i, entry in enumerate(ROW_LOADS[2:]):
-            load_rows(dist_rows, distance, "dist", *entry)
-            load_rows(vel_rows, velocity, "vel", *entry)
-            if i == 0:
-                load_words(*WORD_LOADS[2])
-
-        nc.gpsimd.tensor_copy(out=taper_f[:], in_=taper_bf[:])
-        nc.gpsimd.tensor_copy(out=back_f[:], in_=back_bf[:])
+        load_rows(vel_rows, velocity, "vel", 0)
+        load_rows(vel_rows, velocity, "vel", 1)
+        load_rows(vel_rows, velocity, "vel", 2)
+        load_words(*WORD_LOADS[2])
+        for k in range(3, AHEAD + 1):
+            load_rows(dist_rows, distance, "dist", k)
+            load_rows(vel_rows, velocity, "vel", k)
 
         nc.vector.tensor_copy(out=har_sc[:], in_=har_sc_raw[:].rearrange("p g (m t) -> p g t m", t=4))
         har_view = har_raw[:].rearrange("p g (m t b) -> p g t m b", t=4, b=2)
@@ -316,99 +317,106 @@ def tile_radar_azimuth_harmonic_residuals_k5_kernel(
                 out=har_codes[:, :, t, :].rearrange("p g (m b) -> p g m b", b=2), in_=har_view[:, :, t, :, :]
             )
         square(0)
+        nc.scalar.copy(out=taper_f[:], in_=taper_bf[:])
         gaussian(0)
         for t in range(4):
             project(*CHUNKS[0], t)
         for t in range(4):
             project(*CHUNKS[1], t)
-        if HEAD_S:
-            group_refit(1, True)
-        group_refit(0, False)
+        group_refit(0)
+        square(1)
         for t in range(4):
             taper_slot(*CHUNKS[0], t)
-        for t in range(4):
-            taper_slot(*CHUNKS[1], t)
-        for t in range(4):
-            project(*CHUNKS[2], t)
         quantize_refit(0)
-        if not HEAD_S:
-            group_refit(1, False)
+        group_refit(1)
         group_c(*CHUNKS[0])
         quantize_refit(1)
         quantize_c(*CHUNKS[0])
+        gaussian(1)
+        for t in range(4):
+            taper_slot(*CHUNKS[1], t)
+        refit_rings(0)
+        for t in range(4):
+            project(*CHUNKS[2], t)
         group_c(*CHUNKS[1])
-        for g in range(GROUPS):
-            refit_rings(0, g)
+        square(2)
         for t in range(4):
             taper_slot(*CHUNKS[2], t)
         quantize_c(*CHUNKS[1])
+        refit_rings(1)
         for t in range(2):
             project(*CHUNKS[3], t)
-        for g in range(GROUPS):
-            refit_rings(1, g)
-        subtract(0, 0)
-        group_c(*CHUNKS[2])
-        subtract(0, 1)
-        quantize_c(*CHUNKS[2])
+        subtract(0)
         for t in range(2):
             taper_slot(*CHUNKS[3], t)
-        for t in range(2, 4):
-            project(*CHUNKS[3], t)
+        gaussian(2)
 
-        extras = {}
-        for first, count in CHUNKS[3:]:
-            extras.setdefault(first - 4 + (first == 4), []).append((group_c, (first, count)))
-            extras.setdefault(first - 3, []).append((quantize_c, (first, count)))
-        for first, count in PLANE_SETS[:-1]:
-            ready = first + count + (2 if first < 8 else 1)
-            for g in range(GROUPS):
-                at = ready + g if count == 4 else ready
-                extras.setdefault(at, []).append((quantize_y, (first, count, g)))
+        early = {0: CHUNKS[2], 1: CHUNKS[3], 3: CHUNKS[4], 5: CHUNKS[5]}
+        late = {3: [(0, 4, 0)], 4: [(0, 4, 1)], 5: [(4, 4, 0)], 6: [(4, 4, 1), (8, 2, 0), (8, 2, 1)]}
 
-        last = TILES - 1
-        for s in range(last):
-            if s + 8 < TILES and s > 0:
-                project(8 + 4 * (s // 4), 4, s % 4)
-            if s + 2 < TILES:
-                for g in range(GROUPS):
-                    refit_rings(s + 2, g)
-            if s >= 1:
-                turn(s - 1)
-            square(s + 1)
-            subtract(s + 1, 0)
-            weigh(s)
-            round_gpsimd(s)
-            if s == 0:
-                taper_slot(*CHUNKS[3], 2)
-                project(8, 4, 0)
-            if s >= 2:
-                gather(s - 2)
-            gaussian(s + 1)
-            subtract(s + 1, 1)
-            round_vector(s)
-            if s == 0:
-                taper_slot(*CHUNKS[3], 3)
-            if s + 8 < TILES:
-                taper_slot(8 + 4 * (s // 4), 4, s % 4)
-            round_scalar(s)
-            for fn, args in extras.get(s, []):
-                fn(*args)
+        last = len(UNITS) - 1
+        for k in range(last):
+            if k >= 1:
+                for j in reversed(range(UNITS[k - 1][1])):
+                    turn(k - 1, j)
+            if k >= 1:
+                refit_rings(k + 1)
+            slots = [(8 + 4 * ((k - 1) // 2), 4, 2 * ((k - 1) % 2) + i) for i in range(2)] if 1 <= k < 5 else []
+            if k == 0:
+                slots = [(4, 4, 2), (4, 4, 3)]
+            for slot in slots:
+                project(*slot)
+            if k == 0:
+                for slot in slots:
+                    taper_slot(*slot)
+                slots = []
+            ahead = k + LEAD
+            weights = 3 <= ahead <= last
+            if weights:
+                square(ahead)
+            weigh(k)
+            round_gpsimd(k)
+            subtract(k + 1)
+            if k + AHEAD + 1 <= last:
+                load_rows(dist_rows, distance, "dist", k + AHEAD + 1)
+                load_rows(vel_rows, velocity, "vel", k + AHEAD + 1)
+            if k >= 1:
+                first, count = UNITS[k - 1]
+                for j in range(count):
+                    gather(first + j, not (k in V_GATHER and j == 0))
+            if weights:
+                gaussian(ahead)
+            for slot in slots:
+                taper_slot(*slot)
+            round_rest(k, False)
+            round_rest(k, True)
+            if k in early:
+                group_c(*early[k])
+            for args in late.get(k, []):
+                quantize_y(*args)
+            if k in early:
+                quantize_c(*early[k])
 
-        turn(last - 1)
-        gather(last - 2)
-        weigh(last, (0,))
-        gather(last - 1)
-        weigh(last, (1,))
-        round_half(last, 0)
-        turn(last, (0,))
-        round_half(last, 1)
-        turn(last, (1,))
-        for s in (last, last + 1):
-            for fn, args in extras.get(s, []):
-                fn(*args)
+        for j in reversed(range(2)):
+            turn(last - 1, j)
+        weigh(last, slice(0, 1))
+        round_part(last, 0, 2 * P, True)
+        for j in range(2):
+            gather(12 + j, True)
         for g in range(GROUPS):
-            gather(last, (g,))
-            quantize_y(last, 1, g)
+            weigh(last, slice(1, 2), slice(512 * g, 512 * (g + 1)))
+        turn(last, 0, tag="fit", bufs=4)
+        for g in range(GROUPS):
+            round_part(last, P * (2 + g), P * (3 + g), False)
+        gather(14, True)
+        turn(last, 1, tag="fit", bufs=4)
+        for g in range(GROUPS):
+            quantize_y(10, 2, g)
+        quantize_y(12, 2, 0)
+        gather(15, False)
+        quantize_y(12, 2, 1)
+        for g in range(GROUPS):
+            quantize_y(14, 2, g)
 
         for q in range(4):
             nc.sync.dma_start(

@@ -22,12 +22,15 @@ GROUPS = A // 512
 CHUNKS = [(0, 1), (1, 1), (2, 2), (4, 4), (8, 4), (12, 4)]
 UNITS = [(0, 1), (1, 1), (2, 2), (4, 2), (6, 2), (8, 2), (10, 2), (12, 2), (14, 2)]
 PLANE_SETS = [(0, 4), (4, 4), (8, 2), (10, 2), (12, 2), (14, 2)]
-WORD_LOADS = [(0, 2), (2, 6), (8, 8)]
-G_SHARE = 224
-S_CAST = ()
+WORD_LOADS = [(0, 4), (4, 4), (8, 8)]
+G_SHARE = 768
+S_CAST = (6, 7)
 V_GATHER = ()
 AHEAD = 4
-LEAD = 1
+TAIL_S = True
+IL_EARLY = (0,)
+PLAN = "s0 x0 s1 t||x1||S|X"
+ORDER = "hw hs e0 r0 e1 vs w0 r1 tp bg w1 v0 d1 v1 w2 d2 v2 d3 v3 d4 v4"
 
 
 def tile_radar_azimuth_harmonic_residuals_k5_kernel(
@@ -49,7 +52,6 @@ def tile_radar_azimuth_harmonic_residuals_k5_kernel(
         taper_bf = keep.tile([P, 4], BF16, name="taper_bf")
         back_bf = keep.tile([P, 4], BF16, name="back_bf")
         taper_f = keep.tile([P, 4], F32, name="taper_f")
-        warm = keep.tile([P, 1], F32, name="warm")
         y_sc = keep.tile([P, GROUPS, R], U8, name="y_sc", align_bytes=64)
 
         vel_codes = {}
@@ -88,13 +90,12 @@ def tile_radar_azimuth_harmonic_residuals_k5_kernel(
             )
             vel_codes[first] = t
 
-        def load_rows(store, src, label, k):
-            first, count = UNITS[k]
-            t = flow.tile([P, count, A], BF16, name=label, tag=label, bufs=AHEAD + 1)
-            nc.sync.dma_start(
-                out=t[:], in_=src[P * first : P * (first + count), :].rearrange("(j p) a -> p j a", p=P)
-            )
-            store[k] = t
+        def load_rows(store, src, label, pair, tiles=slice(None)):
+            if pair not in store:
+                t = flow.tile([P, 2, A], BF16, name=label, tag=label, bufs=AHEAD + 1)
+                store[pair] = t
+            rows = src[2 * P * pair : 2 * P * (pair + 1), :].rearrange("(j p) a -> p j a", p=P)
+            nc.sync.dma_start(out=store[pair][:, tiles, :], in_=rows[:, tiles, :])
 
         def load_refit(g):
             t = keep.tile([P, 4, 512], BF16, name="refit_raw%d" % g)
@@ -119,11 +120,11 @@ def tile_radar_azimuth_harmonic_residuals_k5_kernel(
             )
             refit_q[g] = (codes, scales)
 
-        def project(first, count, t):
+        def project(first, count, t, tag="c_bank"):
             n = P * count
             per_bank = 4 // count
             if t % per_bank == 0:
-                bank = psum.tile([P, 512], F32, name="c_bank", tag="c_bank", bufs=2)
+                bank = psum.tile([P, 512], F32, name="c_bank", tag=tag, bufs=2)
                 c_bank[first, t // per_bank] = bank
             dst = c_bank[first, t // per_bank][:, n * (t % per_bank) : n * (t % per_bank + 1)]
             w_first, w_count = owner(WORD_LOADS, first)
@@ -188,72 +189,80 @@ def tile_radar_azimuth_harmonic_residuals_k5_kernel(
                     )
                     fit[j, g] = bank
 
-        def square(k):
-            t = flow.tile([P, UNITS[k][1], A], F32, name="weight", tag="weight", bufs=3)
-            nc.scalar.activation(out=t[:], in_=dist_rows[k][:], func=ACT.Square)
-            weight[k] = t
+        def square(pair, tiles=slice(None)):
+            if pair not in weight:
+                t = flow.tile([P, 2, A], F32, name="weight", tag="weight", bufs=3)
+                weight[pair] = t
+            nc.scalar.activation(out=weight[pair][:, tiles, :], in_=dist_rows[pair][:, tiles, :], func=ACT.Square)
 
-        def gaussian(k):
-            nc.scalar.activation(out=weight[k][:], in_=weight[k][:], func=ACT.Exp, scale=-1.0)
+        def gaussian(pair, tiles=slice(None)):
+            part = weight[pair][:, tiles, :]
+            nc.scalar.activation(out=part, in_=part, func=ACT.Exp, scale=-1.0)
 
         def subtract(k):
             first, count = UNITS[k]
             t = flow.tile([P, count, A], F32, name="y", tag="y", bufs=4)
             y[k] = t
             for j in range(count):
+                pair, side = divmod(first + j, 2)
                 for g in range(GROUPS):
                     cols = slice(512 * g, 512 * (g + 1))
                     nc.vector.tensor_tensor(
-                        out=t[:, j, cols], in0=vel_rows[k][:, j, cols], in1=fit[first + j, g][:], op=ALU.subtract
+                        out=t[:, j, cols], in0=vel_rows[pair][:, side, cols], in1=fit[first + j, g][:], op=ALU.subtract
                     )
 
         def weigh(k, tiles=slice(None), cols=slice(None)):
             first, count = UNITS[k]
+            pair, side = divmod(first, 2)
             part = y[k][:, tiles, cols]
-            nc.vector.tensor_tensor(out=part, in0=part, in1=weight[k][:, tiles, cols], op=ALU.mult)
+            factor = weight[pair][:, side : side + count, :]
+            nc.vector.tensor_tensor(out=part, in0=part, in1=factor[:, tiles, cols], op=ALU.mult)
             dst = out_0[P * first : P * (first + count), :].rearrange("(j p) a -> p j a", p=P)
             nc.sync.dma_start(out=dst[:, tiles, cols], in_=part)
 
         def round_views(k):
-            count = UNITS[k][1]
             if k not in y_bf:
-                t = flow.tile([P, 2, 2 * P * count, 2], BF16, name="y_bf", tag="y_bf", bufs=2, align_bytes=64)
+                t = flow.tile([P, UNITS[k][1] * A], BF16, name="y_bf", tag="y_bf", bufs=2, align_bytes=64)
                 y_bf[k] = t
-            return y_bf[k][:], y[k][:].rearrange("p j (w u e) -> p u (j w) e", u=2, e=2)
+            return y_bf[k], y[k][:].rearrange("p j a -> p (j a)")
 
         def split(k):
-            return (G_SHARE if k in S_CAST else 2 * P) * UNITS[k][1]
+            return G_SHARE * UNITS[k][1]
 
         def round_gpsimd(k):
-            if split(k) > 0:
-                dst, src = round_views(k)
-                nc.gpsimd.tensor_scalar(
-                    out=dst[:, :, : split(k), :], in0=src[:, :, : split(k), :],
-                    scalar1=1.0, scalar2=1.0, op0=ALU.mult, op1=ALU.mult,
-                )
+            dst, src = round_views(k)
+            nc.gpsimd.tensor_scalar(
+                out=dst[:, : split(k)], in0=src[:, : split(k)], scalar1=1.0, scalar2=1.0, op0=ALU.mult, op1=ALU.mult
+            )
 
         def round_rest(k, on_scalar):
-            if split(k) < 2 * P * UNITS[k][1] and on_scalar == (k in S_CAST):
-                dst, src = round_views(k)
-                if on_scalar:
-                    nc.scalar.copy(out=dst[:, :, split(k) :, :], in_=src[:, :, split(k) :, :])
-                else:
-                    nc.vector.tensor_copy(out=dst[:, :, split(k) :, :], in_=src[:, :, split(k) :, :])
+            if split(k) < A * UNITS[k][1] and on_scalar == (k in S_CAST):
+                round_part(k, split(k), A * UNITS[k][1], on_scalar)
 
         def round_part(k, lo, hi, on_scalar):
             dst, src = round_views(k)
             if on_scalar:
-                nc.scalar.copy(out=dst[:, :, lo:hi, :], in_=src[:, :, lo:hi, :])
+                nc.scalar.copy(out=dst[:, lo:hi], in_=src[:, lo:hi])
             else:
-                nc.vector.tensor_copy(out=dst[:, :, lo:hi, :], in_=src[:, :, lo:hi, :])
+                nc.vector.tensor_copy(out=dst[:, lo:hi], in_=src[:, lo:hi])
 
-        def turn(k, j, halves=(0, 1), tag="xt", bufs=2):
-            words = y_bf[k][:].rearrange("p u w e -> p u (w e)").bitcast(F32)
+        def round_sorted(k, lo, hi, on_scalar):
+            dst, src = round_views(k)
+            dst = dst[:, lo:hi].rearrange("p (g u m e) -> p g u m e", u=2, m=P, e=2)
+            src = src[:, lo:hi].rearrange("p (g m u e) -> p g u m e", u=2, m=P, e=2)
+            if on_scalar:
+                nc.scalar.copy(out=dst, in_=src)
+            else:
+                nc.vector.tensor_copy(out=dst, in_=src)
+
+        def turn(k, j, halves=(0, 1), tag="xt", bufs=2, in_order=False):
+            words = y_bf[k][:].bitcast(F32)
             bank = psum.tile([P, 4, P], F32, name="xt", tag=tag, bufs=bufs)
             for g in halves:
+                off = 2 * P * (GROUPS * j + g)
                 for u in range(2):
-                    off = P * (GROUPS * j + g)
-                    nc.tensor.transpose(bank[:, 2 * g + u, :], words[:, u, off : off + P], ident[:])
+                    src = words[:, off + P * u : off + P * (u + 1)] if in_order else words[:, off + u : off + 2 * P : 2]
+                    nc.tensor.transpose(bank[:, 2 * g + u, :], src, ident[:])
                 xt[UNITS[k][0] + j, g] = bank
 
         def gather(j, on_scalar, halves=(0, 1)):
@@ -284,102 +293,125 @@ def tile_radar_azimuth_harmonic_residuals_k5_kernel(
                 dst = out_1.rearrange("g p m t -> p g (m t)")[:, :, 4 * P * first : 4 * (P * first + n)]
                 nc.sync.dma_start(out=dst.bitcast(I32), in_=y_codes[first][:].bitcast(I32))
 
-        nc.vector.memset(har_sc_raw[:].rearrange("p g n -> p (g n)").bitcast(I32), 0)
-        nc.vector.memset(vel_sc[:].rearrange("p g n -> p (g n)").bitcast(I32), 0)
-        nc.vector.memset(warm[:], 0.0)
-        nc.gpsimd.dma_start(out=taper_bf[:], in_=taper.rearrange("(p t) -> p t", t=4))
-        nc.gpsimd.dma_start(out=back_bf[:], in_=background.rearrange("(p t) -> p t", t=4))
+        def store_scales(first, count):
+            cols = slice(P * first, P * (first + count))
+            for q in range(4):
+                nc.sync.dma_start(
+                    out=out_2.rearrange("g q m -> q g m")[4 * q : 4 * q + 4, :, cols].bitcast(I32),
+                    in_=y_sc[32 * q : 32 * q + 4, :, cols].bitcast(I32),
+                )
+
+        nc.gpsimd.memset(har_sc_raw[:].rearrange("p g n -> p (g n)").bitcast(I32), 0)
         make_identity(nc, ident[:])
-        nc.scalar.activation(out=warm[:], in_=warm[:], func=ACT.Exp)
+        nc.vector.memset(vel_sc[:].rearrange("p g n -> p (g n)").bitcast(I32), 0)
 
-        nc.sync.dma_start(out=har_raw[:].bitcast(I32), in_=har_words.rearrange("g p n -> p g n").bitcast(I32))
-        load_scale_rows(har_sc_raw, har_scales)
-        load_rows(dist_rows, distance, "dist", 0)
-        load_words(*WORD_LOADS[0])
-        load_refit(0)
-        load_scale_rows(vel_sc, vel_scales)
-        load_rows(dist_rows, distance, "dist", 1)
-        load_refit(1)
-        load_rows(dist_rows, distance, "dist", 2)
-        load_words(*WORD_LOADS[1])
-        load_rows(vel_rows, velocity, "vel", 0)
-        load_rows(vel_rows, velocity, "vel", 1)
-        load_rows(vel_rows, velocity, "vel", 2)
-        load_words(*WORD_LOADS[2])
-        for k in range(3, AHEAD + 1):
-            load_rows(dist_rows, distance, "dist", k)
-            load_rows(vel_rows, velocity, "vel", k)
+        for step in ORDER.split():
+            if step == "hw":
+                nc.sync.dma_start(out=har_raw[:].bitcast(I32), in_=har_words.rearrange("g p n -> p g n").bitcast(I32))
+            elif step == "hs":
+                load_scale_rows(har_sc_raw, har_scales)
+            elif step == "vs":
+                load_scale_rows(vel_sc, vel_scales)
+            elif step == "tp":
+                nc.sync.dma_start(out=taper_bf[:], in_=taper.rearrange("(p t) -> p t", t=4))
+            elif step == "bg":
+                nc.sync.dma_start(out=back_bf[:], in_=background.rearrange("(p t) -> p t", t=4))
+            elif step[0] == "w":
+                load_words(*WORD_LOADS[int(step[1])])
+            elif step[0] == "r":
+                load_refit(int(step[1]))
+            elif step[0] == "e":
+                load_rows(dist_rows, distance, "dist", 0, slice(int(step[1]), int(step[1]) + 1))
+            elif step[0] == "d":
+                load_rows(dist_rows, distance, "dist", int(step[1]))
+            else:
+                load_rows(vel_rows, velocity, "vel", int(step[1]))
 
-        nc.vector.tensor_copy(out=har_sc[:], in_=har_sc_raw[:].rearrange("p g (m t) -> p g t m", t=4))
         har_view = har_raw[:].rearrange("p g (m t b) -> p g t m b", t=4, b=2)
         for t in range(4):
             nc.vector.tensor_copy(
                 out=har_codes[:, :, t, :].rearrange("p g (m b) -> p g m b", b=2), in_=har_view[:, :, t, :, :]
             )
-        square(0)
-        nc.scalar.copy(out=taper_f[:], in_=taper_bf[:])
-        gaussian(0)
+        nc.vector.tensor_copy(out=har_sc[:], in_=har_sc_raw[:].rearrange("p g (m t) -> p g t m", t=4))
+        def scalar_plan(words):
+            for word in words.split():
+                if word[0] == "s":
+                    square(0, slice(int(word[1]), int(word[1]) + 1))
+                elif word[0] == "x":
+                    gaussian(0, slice(int(word[1]), int(word[1]) + 1))
+                elif word == "S":
+                    square(1)
+                elif word == "X":
+                    gaussian(1)
+                elif word == "t":
+                    nc.scalar.copy(out=taper_f[:], in_=taper_bf[:])
+
+        plan = PLAN.split("|")
         for t in range(4):
             project(*CHUNKS[0], t)
         for t in range(4):
             project(*CHUNKS[1], t)
+        for t in range(4):
+            project(*CHUNKS[2], t, tag="xt")
+        scalar_plan(plan[0])
         group_refit(0)
-        square(1)
         for t in range(4):
             taper_slot(*CHUNKS[0], t)
+        scalar_plan(plan[1])
         quantize_refit(0)
         group_refit(1)
         group_c(*CHUNKS[0])
         quantize_refit(1)
         quantize_c(*CHUNKS[0])
-        gaussian(1)
         for t in range(4):
             taper_slot(*CHUNKS[1], t)
-        refit_rings(0)
-        for t in range(4):
-            project(*CHUNKS[2], t)
-        group_c(*CHUNKS[1])
-        square(2)
-        for t in range(4):
-            taper_slot(*CHUNKS[2], t)
-        quantize_c(*CHUNKS[1])
-        refit_rings(1)
+        scalar_plan(plan[2])
         for t in range(2):
             project(*CHUNKS[3], t)
+        refit_rings(0)
+        group_c(*CHUNKS[1])
+        for t in range(4):
+            taper_slot(*CHUNKS[2], t)
+        scalar_plan(plan[3])
+        quantize_c(*CHUNKS[1])
+        refit_rings(1)
         subtract(0)
         for t in range(2):
             taper_slot(*CHUNKS[3], t)
-        gaussian(2)
+        for t in range(2, 4):
+            project(*CHUNKS[3], t)
+        scalar_plan(plan[4])
+        for t in range(2, 4):
+            taper_slot(*CHUNKS[3], t)
+        scalar_plan(plan[5])
 
         early = {0: CHUNKS[2], 1: CHUNKS[3], 3: CHUNKS[4], 5: CHUNKS[5]}
         late = {3: [(0, 4, 0)], 4: [(0, 4, 1)], 5: [(4, 4, 0)], 6: [(4, 4, 1), (8, 2, 0), (8, 2, 1)]}
 
         last = len(UNITS) - 1
         for k in range(last):
+            if k >= 1 and k - 1 not in early:
+                refit_rings(k + 1)
             if k >= 1:
                 for j in reversed(range(UNITS[k - 1][1])):
                     turn(k - 1, j)
-            if k >= 1:
+            if k - 1 in early:
                 refit_rings(k + 1)
             slots = [(8 + 4 * ((k - 1) // 2), 4, 2 * ((k - 1) % 2) + i) for i in range(2)] if 1 <= k < 5 else []
-            if k == 0:
-                slots = [(4, 4, 2), (4, 4, 3)]
             for slot in slots:
                 project(*slot)
-            if k == 0:
-                for slot in slots:
-                    taper_slot(*slot)
-                slots = []
-            ahead = k + LEAD
-            weights = 3 <= ahead <= last
+            ahead = k
+            weights = 2 <= ahead
             if weights:
                 square(ahead)
+            if k in IL_EARLY:
+                group_c(*early[k])
             weigh(k)
             round_gpsimd(k)
             subtract(k + 1)
-            if k + AHEAD + 1 <= last:
-                load_rows(dist_rows, distance, "dist", k + AHEAD + 1)
-                load_rows(vel_rows, velocity, "vel", k + AHEAD + 1)
+            if k >= 1 and k + AHEAD < TILES // 2:
+                load_rows(dist_rows, distance, "dist", k + AHEAD)
+                load_rows(vel_rows, velocity, "vel", k + AHEAD)
             if k >= 1:
                 first, count = UNITS[k - 1]
                 for j in range(count):
@@ -390,36 +422,35 @@ def tile_radar_azimuth_harmonic_residuals_k5_kernel(
                 taper_slot(*slot)
             round_rest(k, False)
             round_rest(k, True)
-            if k in early:
+            if k in IL_EARLY:
+                quantize_c(*early[k])
+            elif k in early:
                 group_c(*early[k])
             for args in late.get(k, []):
                 quantize_y(*args)
-            if k in early:
+            if k in early and k not in IL_EARLY:
                 quantize_c(*early[k])
+            if k == last - 1:
+                store_scales(0, 10)
 
         for j in reversed(range(2)):
             turn(last - 1, j)
         weigh(last, slice(0, 1))
-        round_part(last, 0, 2 * P, True)
+        round_sorted(last, 0, A, True)
         for j in range(2):
             gather(12 + j, True)
         for g in range(GROUPS):
             weigh(last, slice(1, 2), slice(512 * g, 512 * (g + 1)))
-        turn(last, 0, tag="fit", bufs=4)
+        turn(last, 0, tag="fit", bufs=4, in_order=True)
         for g in range(GROUPS):
-            round_part(last, P * (2 + g), P * (3 + g), False)
+            round_sorted(last, A + 512 * g, A + 512 * (g + 1), False)
         gather(14, True)
-        turn(last, 1, tag="fit", bufs=4)
+        turn(last, 1, tag="fit", bufs=4, in_order=True)
         for g in range(GROUPS):
             quantize_y(10, 2, g)
         quantize_y(12, 2, 0)
-        gather(15, False)
+        gather(15, TAIL_S)
         quantize_y(12, 2, 1)
         for g in range(GROUPS):
             quantize_y(14, 2, g)
-
-        for q in range(4):
-            nc.sync.dma_start(
-                out=out_2.rearrange("g q m -> q g m")[4 * q : 4 * q + 4, :, :].bitcast(I32),
-                in_=y_sc[32 * q : 32 * q + 4, :, :].bitcast(I32),
-            )
+        store_scales(10, 6)

@@ -17,20 +17,26 @@ ACT = mybir.ActivationFunctionType
 ALU = mybir.AluOpType
 
 P = 128
+PACK = 4
+HALF = 512
+HALVES = A // HALF
 TILES = R // P
-GROUPS = A // 512
-CHUNKS = [(0, 1), (1, 1), (2, 2), (4, 4), (8, 4), (12, 4)]
-UNITS = [(0, 1), (1, 1), (2, 2), (4, 2), (6, 2), (8, 2), (10, 2), (12, 2), (14, 2)]
-PLANE_SETS = [(0, 4), (4, 4), (8, 2), (10, 2), (12, 2), (14, 2)]
+PAIRS = TILES // 2
+
+CHUNKS = [(0, 1), (1, 1), (2, 2)] + [(first, 4) for first in range(4, TILES, 4)]
+UNITS = [(0, 1), (1, 1)] + [(first, 2) for first in range(2, TILES, 2)]
+PLANE_SETS = [(0, 4), (4, 4)] + [(first, 2) for first in range(8, TILES, 2)]
 WORD_LOADS = [(0, 4), (4, 4), (8, 8)]
-G_SHARE = 768
-S_CAST = (6, 7)
-V_GATHER = ()
-AHEAD = 4
-TAIL_S = True
-IL_EARLY = (0,)
-PLAN = "s0 x0 s1 t||x1||S|X"
-ORDER = "hw hs e0 r0 e1 vs w0 r1 tp bg w1 v0 d1 v1 w2 d2 v2 d3 v3 d4 v4"
+ROW_BUFS = 5
+FIT_BANKS = 4
+
+
+def owner(table, tile):
+    return [entry for entry in table if entry[0] <= tile < entry[0] + entry[1]][0]
+
+
+def unit_of(tile):
+    return UNITS.index(owner(UNITS, tile))
 
 
 def tile_radar_azimuth_harmonic_residuals_k5_kernel(
@@ -44,36 +50,25 @@ def tile_radar_azimuth_harmonic_residuals_k5_kernel(
         ctx.enter_context(tc.manual_schedule())
 
         ident = keep.tile([P, P], F32, name="ident")
-        har_raw = keep.tile([P, GROUPS, 2 * H], U8, name="har_raw", align_bytes=64)
-        har_sc_raw = keep.tile([P, GROUPS, H], U8, name="har_sc_raw", align_bytes=64)
-        har_codes = keep.tile([P, GROUPS, 4, 2 * P], U8, name="har_codes", align_bytes=64)
-        har_sc = keep.tile([P, GROUPS, 4, P], U8, name="har_sc", align_bytes=64)
-        vel_sc = keep.tile([P, GROUPS, R], U8, name="vel_sc", align_bytes=64)
-        taper_bf = keep.tile([P, 4], BF16, name="taper_bf")
-        back_bf = keep.tile([P, 4], BF16, name="back_bf")
-        taper_f = keep.tile([P, 4], F32, name="taper_f")
-        y_sc = keep.tile([P, GROUPS, R], U8, name="y_sc", align_bytes=64)
+        har_raw = keep.tile([P, HALVES, 2 * H], U8, name="har_raw", align_bytes=64)
+        har_sc_raw = keep.tile([P, HALVES, H], U8, name="har_sc_raw", align_bytes=64)
+        har_codes = keep.tile([P, HALVES, PACK, 2 * P], U8, name="har_codes", align_bytes=64)
+        har_sc = keep.tile([P, HALVES, PACK, P], U8, name="har_sc", align_bytes=64)
+        vel_sc = keep.tile([P, HALVES, R], U8, name="vel_sc", align_bytes=64)
+        taper_bf = keep.tile([P, PACK], BF16, name="taper_bf")
+        back_bf = keep.tile([P, PACK], BF16, name="back_bf")
+        taper_f = keep.tile([P, PACK], F32, name="taper_f")
+        y_sc = keep.tile([P, HALVES, R], U8, name="y_sc", align_bytes=64)
 
         vel_codes = {}
-        vel_rows = {}
-        dist_rows = {}
-        refit_raw = {}
-        refit_grp = {}
-        refit_q = {}
+        vel_rows, dist_rows, weight = {}, {}, {}
+        refit_raw, refit_words, refit_mx = {}, {}, {}
         c_bank = {}
-        c_slots = {}
-        c_grp = {}
-        c_q = {}
+        c_slots, c_words, c_mx = {}, {}, {}
         fit = {}
-        weight = {}
-        y = {}
-        y_bf = {}
-        xt = {}
-        q_in = {}
-        y_codes = {}
-
-        def owner(table, j):
-            return [entry for entry in table if entry[0] <= j < entry[0] + entry[1]][0]
+        y, y_bf = {}, {}
+        turned = {}
+        y_words, y_codes = {}, {}
 
         def load_scale_rows(plane, rows):
             for q in range(4):
@@ -83,132 +78,139 @@ def tile_radar_azimuth_harmonic_residuals_k5_kernel(
                 )
 
         def load_words(first, count):
-            t = keep.tile([P, GROUPS, 2 * P * count], U8, name="vel_codes%d" % first, align_bytes=64)
+            codes = keep.tile([P, HALVES, 2 * P * count], U8, name="vel_codes%d" % first, align_bytes=64)
             nc.sync.dma_start(
-                out=t[:].bitcast(I32),
+                out=codes[:].bitcast(I32),
                 in_=vel_words.rearrange("g p n -> p g n")[:, :, 2 * P * first : 2 * P * (first + count)].bitcast(I32),
             )
-            vel_codes[first] = t
+            vel_codes[first] = codes
 
-        def load_rows(store, src, label, pair, tiles=slice(None)):
+        def load_rows(store, src, label, pair, sides=slice(None)):
             if pair not in store:
-                t = flow.tile([P, 2, A], BF16, name=label, tag=label, bufs=AHEAD + 1)
-                store[pair] = t
+                store[pair] = flow.tile([P, 2, A], BF16, name=label, tag=label, bufs=ROW_BUFS)
             rows = src[2 * P * pair : 2 * P * (pair + 1), :].rearrange("(j p) a -> p j a", p=P)
-            nc.sync.dma_start(out=store[pair][:, tiles, :], in_=rows[:, tiles, :])
+            nc.sync.dma_start(out=store[pair][:, sides, :], in_=rows[:, sides, :])
+
+        def load_distance(pair, sides=slice(None)):
+            load_rows(dist_rows, distance, "dist", pair, sides)
+
+        def load_velocity(pair):
+            load_rows(vel_rows, velocity, "vel", pair)
 
         def load_refit(g):
-            t = keep.tile([P, 4, 512], BF16, name="refit_raw%d" % g)
-            nc.sync.dma_start(out=t[:], in_=refit[:, 512 * g : 512 * (g + 1)].rearrange("(p t) a -> p t a", t=4))
-            refit_raw[g] = t
+            raw = keep.tile([P, PACK, HALF], BF16, name="refit_raw%d" % g)
+            nc.sync.dma_start(out=raw[:], in_=refit[:, HALF * g : HALF * (g + 1)].rearrange("(p t) a -> p t a", t=PACK))
+            refit_raw[g] = raw
 
         def interleave(dst, src):
             nc.vector.tensor_copy(
                 out=dst.rearrange("p (c i) t -> p c t i", i=4), in_=src.rearrange("p t (c i) -> p c t i", i=4)
             )
 
-        def group_refit(g):
-            t = keep.tile([P, 512, 4], BF16, name="refit_grp%d" % g, align_bytes=64)
-            interleave(t[:], refit_raw[g][:])
-            refit_grp[g] = t
+        def quantize_words(words, label):
+            width = words.shape[1]
+            codes = keep.tile([P, width], U32, name=label + "_codes", align_bytes=64)
+            scales = keep.tile([P, width], U8, name=label + "_sc", align_bytes=64)
+            nc.vector.quantize_mx(
+                out=codes[:].bitcast(FP8X4), scales=scales[:], in_=words[:].rearrange("p c t -> p (c t)")
+            )
+            return codes, scales
+
+        def interleave_refit(g):
+            refit_words[g] = keep.tile([P, HALF, PACK], BF16, name="refit_words%d" % g, align_bytes=64)
+            interleave(refit_words[g][:], refit_raw[g][:])
 
         def quantize_refit(g):
-            codes = keep.tile([P, 512], U32, name="refit_codes%d" % g, align_bytes=64)
-            scales = keep.tile([P, 512], U8, name="refit_sc%d" % g, align_bytes=64)
-            nc.vector.quantize_mx(
-                out=codes[:].bitcast(FP8X4), scales=scales[:], in_=refit_grp[g][:].rearrange("p a t -> p (a t)")
-            )
-            refit_q[g] = (codes, scales)
+            refit_mx[g] = quantize_words(refit_words[g], "refit%d" % g)
 
-        def project(first, count, t, tag="c_bank"):
-            n = P * count
-            per_bank = 4 // count
-            if t % per_bank == 0:
-                bank = psum.tile([P, 512], F32, name="c_bank", tag=tag, bufs=2)
-                c_bank[first, t // per_bank] = bank
-            dst = c_bank[first, t // per_bank][:, n * (t % per_bank) : n * (t % per_bank + 1)]
-            w_first, w_count = owner(WORD_LOADS, first)
-            off = P * (first - w_first)
-            for g in range(GROUPS):
-                nc.tensor.matmul_mx(
-                    out=dst,
-                    lhsT=har_codes[:, g, t, :].bitcast(FP4X4),
-                    lhsT_scale=har_sc[:, g, t, :],
-                    rhs=vel_codes[w_first][:, g, 2 * off : 2 * (off + n)].bitcast(FP4X4),
-                    rhs_scale=vel_sc[:, g, P * first : P * first + n],
-                    start=(g == 0),
-                    stop=(g == GROUPS - 1),
+        def slot_columns(chunk, t):
+            first, count = chunk
+            per_bank = PACK // count
+            start = P * count * (t % per_bank)
+            return c_bank[first, t // per_bank][:, start : start + P * count]
+
+        def project(chunk, slots, tag="c_bank"):
+            first, count = chunk
+            per_bank = PACK // count
+            load_first = owner(WORD_LOADS, first)[0]
+            start = 2 * P * (first - load_first)
+            for t in slots:
+                if t % per_bank == 0:
+                    c_bank[first, t // per_bank] = psum.tile([P, HALF], F32, name="c_bank", tag=tag, bufs=2)
+                for g in range(HALVES):
+                    nc.tensor.matmul_mx(
+                        out=slot_columns(chunk, t),
+                        lhsT=har_codes[:, g, t, :].bitcast(FP4X4),
+                        lhsT_scale=har_sc[:, g, t, :],
+                        rhs=vel_codes[load_first][:, g, start : start + 2 * P * count].bitcast(FP4X4),
+                        rhs_scale=vel_sc[:, g, P * first : P * (first + count)],
+                        start=(g == 0),
+                        stop=(g == HALVES - 1),
+                    )
+
+        def apply_taper(chunk, slots):
+            first, count = chunk
+            for t in slots:
+                if t == 0:
+                    c_slots[first] = flow.tile([P, PACK, P * count], BF16, name="c_slots", tag="c_slots", bufs=2)
+                nc.scalar.activation(
+                    out=c_slots[first][:, t, :],
+                    in_=slot_columns(chunk, t),
+                    func=ACT.Identity,
+                    scale=taper_f[:, t : t + 1],
+                    bias=back_bf[:, t : t + 1],
                 )
 
-        def taper_slot(first, count, t):
-            n = P * count
-            per_bank = 4 // count
-            if t == 0:
-                slots = flow.tile([P, 4, n], BF16, name="c_slots", tag="c_slots", bufs=2)
-                c_slots[first] = slots
-            src = c_bank[first, t // per_bank][:, n * (t % per_bank) : n * (t % per_bank + 1)]
-            nc.scalar.activation(
-                out=c_slots[first][:, t, :],
-                in_=src,
-                func=ACT.Identity,
-                scale=taper_f[:, t : t + 1],
-                bias=back_bf[:, t : t + 1],
+        def interleave_c(chunk):
+            first, count = chunk
+            c_words[first] = flow.tile(
+                [P, P * count, PACK], BF16, name="c_words", tag="c_words", bufs=2, align_bytes=64
             )
+            interleave(c_words[first][:], c_slots[first][:])
 
-        def group_c(first, count):
-            n = P * count
-            t = flow.tile([P, n, 4], BF16, name="c_grp", tag="c_grp", bufs=2, align_bytes=64)
-            interleave(t[:], c_slots[first][:])
-            c_grp[first] = t
+        def quantize_c(chunk):
+            c_mx[chunk[0]] = quantize_words(c_words[chunk[0]], "c%d" % chunk[0])
 
-        def quantize_c(first, count):
-            n = P * count
-            codes = keep.tile([P, n], U32, name="c_codes%d" % first, align_bytes=64)
-            scales = keep.tile([P, n], U8, name="c_sc%d" % first, align_bytes=64)
-            nc.vector.quantize_mx(
-                out=codes[:].bitcast(FP8X4), scales=scales[:], in_=c_grp[first][:].rearrange("p r t -> p (r t)")
-            )
-            c_q[first] = (codes, scales)
-
-        def refit_rings(k):
-            unit_first, unit_count = UNITS[k]
-            for j in range(unit_first, unit_first + unit_count):
-                first, count = owner(CHUNKS, j)
-                codes, scales = c_q[first]
-                cols = slice(P * (j - first), P * (j - first + 1))
-                for g in reversed(range(GROUPS)):
-                    bank = psum.tile([P, 512], F32, name="fit", tag="fit", bufs=4)
+        def refit_rings(k, backwards=False, halves=(1, 0)):
+            tiles = range(UNITS[k][0], UNITS[k][0] + UNITS[k][1])
+            for j in reversed(tiles) if backwards else tiles:
+                first = owner(CHUNKS, j)[0]
+                codes, scales = c_mx[first]
+                rings = slice(P * (j - first), P * (j - first + 1))
+                for g in halves:
+                    fit[j, g] = psum.tile([P, HALF], F32, name="fit", tag="fit", bufs=FIT_BANKS)
                     nc.tensor.matmul_mx(
-                        out=bank[:],
-                        lhsT=codes[:, cols].bitcast(FP8X4),
-                        lhsT_scale=scales[:, cols],
-                        rhs=refit_q[g][0][:].bitcast(FP8X4),
-                        rhs_scale=refit_q[g][1][:],
+                        out=fit[j, g][:],
+                        lhsT=codes[:, rings].bitcast(FP8X4),
+                        lhsT_scale=scales[:, rings],
+                        rhs=refit_mx[g][0][:].bitcast(FP8X4),
+                        rhs_scale=refit_mx[g][1][:],
                         start=True,
                         stop=True,
                     )
-                    fit[j, g] = bank
 
-        def square(pair, tiles=slice(None)):
+        def square(pair, sides=slice(None)):
             if pair not in weight:
-                t = flow.tile([P, 2, A], F32, name="weight", tag="weight", bufs=3)
-                weight[pair] = t
-            nc.scalar.activation(out=weight[pair][:, tiles, :], in_=dist_rows[pair][:, tiles, :], func=ACT.Square)
+                weight[pair] = flow.tile([P, 2, A], F32, name="weight", tag="weight", bufs=3)
+            nc.scalar.activation(out=weight[pair][:, sides, :], in_=dist_rows[pair][:, sides, :], func=ACT.Square)
 
-        def gaussian(pair, tiles=slice(None)):
-            part = weight[pair][:, tiles, :]
+        def gaussian(pair, sides=slice(None)):
+            part = weight[pair][:, sides, :]
             nc.scalar.activation(out=part, in_=part, func=ACT.Exp, scale=-1.0)
 
-        def subtract(k):
+        def subtract(k, halves=(0, 1)):
             first, count = UNITS[k]
-            t = flow.tile([P, count, A], F32, name="y", tag="y", bufs=4)
-            y[k] = t
+            if k not in y:
+                y[k] = flow.tile([P, count, A], F32, name="y", tag="y", bufs=4)
             for j in range(count):
                 pair, side = divmod(first + j, 2)
-                for g in range(GROUPS):
-                    cols = slice(512 * g, 512 * (g + 1))
+                for g in halves:
+                    cols = slice(HALF * g, HALF * (g + 1))
                     nc.vector.tensor_tensor(
-                        out=t[:, j, cols], in0=vel_rows[pair][:, side, cols], in1=fit[first + j, g][:], op=ALU.subtract
+                        out=y[k][:, j, cols],
+                        in0=vel_rows[pair][:, side, cols],
+                        in1=fit[first + j, g][:],
+                        op=ALU.subtract,
                     )
 
         def weigh(k, tiles=slice(None), cols=slice(None)):
@@ -222,235 +224,202 @@ def tile_radar_azimuth_harmonic_residuals_k5_kernel(
 
         def round_views(k):
             if k not in y_bf:
-                t = flow.tile([P, UNITS[k][1] * A], BF16, name="y_bf", tag="y_bf", bufs=2, align_bytes=64)
-                y_bf[k] = t
+                y_bf[k] = flow.tile([P, UNITS[k][1] * A], BF16, name="y_bf", tag="y_bf", bufs=2, align_bytes=64)
             return y_bf[k], y[k][:].rearrange("p j a -> p (j a)")
 
-        def split(k):
-            return G_SHARE * UNITS[k][1]
+        def plain_columns(k):
+            return A * UNITS[k][1] - HALF if k < len(UNITS) - 1 else 0
 
-        def round_gpsimd(k):
+        def round_plain(k):
             dst, src = round_views(k)
+            cols = slice(0, plain_columns(k))
             nc.gpsimd.tensor_scalar(
-                out=dst[:, : split(k)], in0=src[:, : split(k)], scalar1=1.0, scalar2=1.0, op0=ALU.mult, op1=ALU.mult
+                out=dst[:, cols], in0=src[:, cols], scalar1=1.0, scalar2=1.0, op0=ALU.mult, op1=ALU.mult
             )
 
-        def round_rest(k, on_scalar):
-            if split(k) < A * UNITS[k][1] and on_scalar == (k in S_CAST):
-                round_part(k, split(k), A * UNITS[k][1], on_scalar)
-
-        def round_part(k, lo, hi, on_scalar):
+        def round_sorted(k, start, width, copy):
             dst, src = round_views(k)
-            if on_scalar:
-                nc.scalar.copy(out=dst[:, lo:hi], in_=src[:, lo:hi])
-            else:
-                nc.vector.tensor_copy(out=dst[:, lo:hi], in_=src[:, lo:hi])
+            copy(
+                out=dst[:, start : start + width].rearrange("p (g u m e) -> p g u m e", u=2, m=P, e=2),
+                in_=src[:, start : start + width].rearrange("p (g m u e) -> p g u m e", u=2, m=P, e=2),
+            )
 
-        def round_sorted(k, lo, hi, on_scalar):
-            dst, src = round_views(k)
-            dst = dst[:, lo:hi].rearrange("p (g u m e) -> p g u m e", u=2, m=P, e=2)
-            src = src[:, lo:hi].rearrange("p (g m u e) -> p g u m e", u=2, m=P, e=2)
-            if on_scalar:
-                nc.scalar.copy(out=dst, in_=src)
-            else:
-                nc.vector.tensor_copy(out=dst, in_=src)
-
-        def turn(k, j, halves=(0, 1), tag="xt", bufs=2, in_order=False):
+        def turn(k, j, tag="turned", bufs=2):
             words = y_bf[k][:].bitcast(F32)
-            bank = psum.tile([P, 4, P], F32, name="xt", tag=tag, bufs=bufs)
-            for g in halves:
-                off = 2 * P * (GROUPS * j + g)
+            bank = psum.tile([P, 2 * HALVES, P], F32, name="turned", tag=tag, bufs=bufs)
+            for g in range(HALVES):
+                start = 2 * P * (HALVES * j + g)
                 for u in range(2):
-                    src = words[:, off + P * u : off + P * (u + 1)] if in_order else words[:, off + u : off + 2 * P : 2]
+                    if 2 * start < plain_columns(k):
+                        src = words[:, start + u : start + 2 * P : 2]
+                    else:
+                        src = words[:, start + P * u : start + P * (u + 1)]
                     nc.tensor.transpose(bank[:, 2 * g + u, :], src, ident[:])
-                xt[UNITS[k][0] + j, g] = bank
+            turned[UNITS[k][0] + j] = bank
 
-        def gather(j, on_scalar, halves=(0, 1)):
+        def gather(j):
             first, count = owner(PLANE_SETS, j)
-            if first not in q_in:
-                t = flow.tile([P, GROUPS, 4 * P * count], BF16, name="q_in", tag="q_in", bufs=4, align_bytes=64)
-                q_in[first] = t
-            gs = slice(halves[0], halves[-1] + 1)
-            words = q_in[first][:].bitcast(F32)[:, gs, 2 * P * (j - first) : 2 * P * (j - first + 1)]
-            dst = words.rearrange("p g (r u) -> p g r u", u=2)
-            src = xt[j, halves[0]][:].rearrange("p (g u) r -> p g r u", u=2)[:, gs]
-            if on_scalar:
-                nc.scalar.copy(out=dst, in_=src)
-            else:
-                nc.vector.tensor_copy(out=dst, in_=src)
+            if first not in y_words:
+                y_words[first] = flow.tile(
+                    [P, HALVES, PACK * P * count], BF16, name="y_words", tag="y_words", bufs=4, align_bytes=64
+                )
+            words = y_words[first][:].bitcast(F32)[:, :, 2 * P * (j - first) : 2 * P * (j - first + 1)]
+            nc.scalar.copy(
+                out=words.rearrange("p g (r u) -> p g r u", u=2),
+                in_=turned[j][:].rearrange("p (g u) r -> p g r u", u=2),
+            )
 
-        def quantize_y(first, count, g):
-            n = P * count
+        def quantize_y(plane_set, g):
+            first, count = plane_set
             if g == 0:
-                t = flow.tile([P, GROUPS, n], U32, name="y_codes", tag="y_codes", bufs=3, align_bytes=64)
-                y_codes[first] = t
+                y_codes[first] = flow.tile(
+                    [P, HALVES, P * count], U32, name="y_codes", tag="y_codes", bufs=3, align_bytes=64
+                )
             nc.vector.quantize_mx(
                 out=y_codes[first][:, g, :].bitcast(FP8X4),
-                scales=y_sc[:, g, P * first : P * first + n],
-                in_=q_in[first][:, g, :],
+                scales=y_sc[:, g, P * first : P * (first + count)],
+                in_=y_words[first][:, g, :],
             )
-            if g == GROUPS - 1:
-                dst = out_1.rearrange("g p m t -> p g (m t)")[:, :, 4 * P * first : 4 * (P * first + n)]
+            if g == HALVES - 1:
+                dst = out_1.rearrange("g p m t -> p g (m t)")[:, :, PACK * P * first : PACK * P * (first + count)]
                 nc.sync.dma_start(out=dst.bitcast(I32), in_=y_codes[first][:].bitcast(I32))
 
-        def store_scales(first, count):
-            cols = slice(P * first, P * (first + count))
+        def store_scales(first, count, queue):
+            rings = slice(P * first, P * (first + count))
             for q in range(4):
-                nc.sync.dma_start(
-                    out=out_2.rearrange("g q m -> q g m")[4 * q : 4 * q + 4, :, cols].bitcast(I32),
-                    in_=y_sc[32 * q : 32 * q + 4, :, cols].bitcast(I32),
+                queue.dma_start(
+                    out=out_2.rearrange("g q m -> q g m")[4 * q : 4 * q + 4, :, rings].bitcast(I32),
+                    in_=y_sc[32 * q : 32 * q + 4, :, rings].bitcast(I32),
                 )
 
         nc.gpsimd.memset(har_sc_raw[:].rearrange("p g n -> p (g n)").bitcast(I32), 0)
         make_identity(nc, ident[:])
         nc.vector.memset(vel_sc[:].rearrange("p g n -> p (g n)").bitcast(I32), 0)
 
-        for step in ORDER.split():
-            if step == "hw":
-                nc.sync.dma_start(out=har_raw[:].bitcast(I32), in_=har_words.rearrange("g p n -> p g n").bitcast(I32))
-            elif step == "hs":
-                load_scale_rows(har_sc_raw, har_scales)
-            elif step == "vs":
-                load_scale_rows(vel_sc, vel_scales)
-            elif step == "tp":
-                nc.sync.dma_start(out=taper_bf[:], in_=taper.rearrange("(p t) -> p t", t=4))
-            elif step == "bg":
-                nc.sync.dma_start(out=back_bf[:], in_=background.rearrange("(p t) -> p t", t=4))
-            elif step[0] == "w":
-                load_words(*WORD_LOADS[int(step[1])])
-            elif step[0] == "r":
-                load_refit(int(step[1]))
-            elif step[0] == "e":
-                load_rows(dist_rows, distance, "dist", 0, slice(int(step[1]), int(step[1]) + 1))
-            elif step[0] == "d":
-                load_rows(dist_rows, distance, "dist", int(step[1]))
-            else:
-                load_rows(vel_rows, velocity, "vel", int(step[1]))
+        side_0, side_1 = slice(0, 1), slice(1, 2)
+        nc.sync.dma_start(out=har_raw[:].bitcast(I32), in_=har_words.rearrange("g p n -> p g n").bitcast(I32))
+        load_scale_rows(har_sc_raw, har_scales)
+        load_distance(0, side_0)
+        load_refit(0)
+        load_distance(0, side_1)
+        load_scale_rows(vel_sc, vel_scales)
+        load_words(*WORD_LOADS[0])
+        load_refit(1)
+        nc.sync.dma_start(out=taper_bf[:], in_=taper.rearrange("(p t) -> p t", t=PACK))
+        nc.sync.dma_start(out=back_bf[:], in_=background.rearrange("(p t) -> p t", t=PACK))
+        load_words(*WORD_LOADS[1])
+        load_velocity(0)
+        load_distance(1)
+        load_velocity(1)
+        load_words(*WORD_LOADS[2])
+        for pair in range(2, ROW_BUFS):
+            load_distance(pair)
+            load_velocity(pair)
 
-        har_view = har_raw[:].rearrange("p g (m t b) -> p g t m b", t=4, b=2)
-        for t in range(4):
-            nc.vector.tensor_copy(
-                out=har_codes[:, :, t, :].rearrange("p g (m b) -> p g m b", b=2), in_=har_view[:, :, t, :, :]
-            )
-        nc.vector.tensor_copy(out=har_sc[:], in_=har_sc_raw[:].rearrange("p g (m t) -> p g t m", t=4))
-        def scalar_plan(words):
-            for word in words.split():
-                if word[0] == "s":
-                    square(0, slice(int(word[1]), int(word[1]) + 1))
-                elif word[0] == "x":
-                    gaussian(0, slice(int(word[1]), int(word[1]) + 1))
-                elif word == "S":
-                    square(1)
-                elif word == "X":
-                    gaussian(1)
-                elif word == "t":
-                    nc.scalar.copy(out=taper_f[:], in_=taper_bf[:])
+        nc.vector.tensor_copy(
+            out=har_codes[:].rearrange("p g t (m b) -> p g t m b", b=2),
+            in_=har_raw[:].rearrange("p g (m t b) -> p g t m b", t=PACK, b=2),
+        )
+        nc.vector.tensor_copy(out=har_sc[:], in_=har_sc_raw[:].rearrange("p g (m t) -> p g t m", t=PACK))
 
-        plan = PLAN.split("|")
-        for t in range(4):
-            project(*CHUNKS[0], t)
-        for t in range(4):
-            project(*CHUNKS[1], t)
-        for t in range(4):
-            project(*CHUNKS[2], t, tag="xt")
-        scalar_plan(plan[0])
-        group_refit(0)
-        for t in range(4):
-            taper_slot(*CHUNKS[0], t)
-        scalar_plan(plan[1])
+        all_slots, low_slots, high_slots = range(PACK), range(2), range(2, PACK)
+        project(CHUNKS[0], all_slots)
+        project(CHUNKS[1], all_slots)
+        project(CHUNKS[2], all_slots, tag="turned")
+        square(0, side_0)
+        gaussian(0, side_0)
+        square(0, side_1)
+        nc.scalar.copy(out=taper_f[:], in_=taper_bf[:])
+        interleave_refit(0)
+        apply_taper(CHUNKS[0], all_slots)
         quantize_refit(0)
-        group_refit(1)
-        group_c(*CHUNKS[0])
+        interleave_refit(1)
+        interleave_c(CHUNKS[0])
+        quantize_c(CHUNKS[0])
+        refit_rings(0, halves=(0,))
         quantize_refit(1)
-        quantize_c(*CHUNKS[0])
-        for t in range(4):
-            taper_slot(*CHUNKS[1], t)
-        scalar_plan(plan[2])
-        for t in range(2):
-            project(*CHUNKS[3], t)
-        refit_rings(0)
-        group_c(*CHUNKS[1])
-        for t in range(4):
-            taper_slot(*CHUNKS[2], t)
-        scalar_plan(plan[3])
-        quantize_c(*CHUNKS[1])
+        apply_taper(CHUNKS[1], all_slots)
+        refit_rings(0, halves=(1,))
+        project(CHUNKS[3], low_slots)
+        interleave_c(CHUNKS[1])
+        apply_taper(CHUNKS[2], all_slots)
+        gaussian(0, side_1)
+        subtract(0, halves=(0,))
+        quantize_c(CHUNKS[1])
         refit_rings(1)
-        subtract(0)
-        for t in range(2):
-            taper_slot(*CHUNKS[3], t)
-        for t in range(2, 4):
-            project(*CHUNKS[3], t)
-        scalar_plan(plan[4])
-        for t in range(2, 4):
-            taper_slot(*CHUNKS[3], t)
-        scalar_plan(plan[5])
-
-        early = {0: CHUNKS[2], 1: CHUNKS[3], 3: CHUNKS[4], 5: CHUNKS[5]}
-        late = {3: [(0, 4, 0)], 4: [(0, 4, 1)], 5: [(4, 4, 0)], 6: [(4, 4, 1), (8, 2, 0), (8, 2, 1)]}
+        interleave_c(CHUNKS[2])
+        subtract(0, halves=(1,))
+        quantize_c(CHUNKS[2])
+        apply_taper(CHUNKS[3], low_slots)
+        project(CHUNKS[3], high_slots)
+        square(1)
+        apply_taper(CHUNKS[3], high_slots)
+        gaussian(1)
 
         last = len(UNITS) - 1
+        quantize_c_at = {unit_of(chunk[0]) - 2: chunk for chunk in CHUNKS[3:]}
+        project_at = {}
+        for chunk in CHUNKS[4:]:
+            project_at[unit_of(chunk[0]) - 4] = (chunk, low_slots)
+            project_at[unit_of(chunk[0]) - 3] = (chunk, high_slots)
+        loop_sets, tail_sets = PLANE_SETS[:-3], PLANE_SETS[-3:]
+        quantize_y_at = {}
+        for first, count in loop_sets:
+            for g in range(HALVES):
+                step = unit_of(first + count - 1) + 1 + (g if count == 4 else 0)
+                quantize_y_at.setdefault(step, []).append(((first, count), g))
+
         for k in range(last):
-            if k >= 1 and k - 1 not in early:
-                refit_rings(k + 1)
             if k >= 1:
+                codes_come_late = k - 1 in quantize_c_at
+                if not codes_come_late:
+                    refit_rings(k + 1, backwards=k > 1)
                 for j in reversed(range(UNITS[k - 1][1])):
                     turn(k - 1, j)
-            if k - 1 in early:
-                refit_rings(k + 1)
-            slots = [(8 + 4 * ((k - 1) // 2), 4, 2 * ((k - 1) % 2) + i) for i in range(2)] if 1 <= k < 5 else []
-            for slot in slots:
-                project(*slot)
-            ahead = k
-            weights = 2 <= ahead
-            if weights:
-                square(ahead)
-            if k in IL_EARLY:
-                group_c(*early[k])
+                if codes_come_late:
+                    refit_rings(k + 1)
+            if k in project_at:
+                project(project_at[k][0], reversed(project_at[k][1]))
+            if k >= 2:
+                square(k)
             weigh(k)
-            round_gpsimd(k)
+            round_plain(k)
             subtract(k + 1)
-            if k >= 1 and k + AHEAD < TILES // 2:
-                load_rows(dist_rows, distance, "dist", k + AHEAD)
-                load_rows(vel_rows, velocity, "vel", k + AHEAD)
+            if k >= 1 and k + ROW_BUFS - 1 < PAIRS:
+                load_distance(k + ROW_BUFS - 1)
+                load_velocity(k + ROW_BUFS - 1)
             if k >= 1:
-                first, count = UNITS[k - 1]
-                for j in range(count):
-                    gather(first + j, not (k in V_GATHER and j == 0))
-            if weights:
-                gaussian(ahead)
-            for slot in slots:
-                taper_slot(*slot)
-            round_rest(k, False)
-            round_rest(k, True)
-            if k in IL_EARLY:
-                quantize_c(*early[k])
-            elif k in early:
-                group_c(*early[k])
-            for args in late.get(k, []):
-                quantize_y(*args)
-            if k in early and k not in IL_EARLY:
-                quantize_c(*early[k])
-            if k == last - 1:
-                store_scales(0, 10)
+                for j in range(UNITS[k - 1][1]):
+                    gather(UNITS[k - 1][0] + j)
+            if k >= 2:
+                gaussian(k)
+            if k in project_at:
+                apply_taper(*project_at[k])
+            round_sorted(k, plain_columns(k), HALF, nc.scalar.copy if k == last - 1 else nc.vector.tensor_copy)
+            if k in quantize_c_at:
+                interleave_c(quantize_c_at[k])
+            for plane_set, g in quantize_y_at.get(k, []):
+                quantize_y(plane_set, g)
+            if k in quantize_c_at:
+                quantize_c(quantize_c_at[k])
+        store_scales(0, tail_sets[0][0], nc.sync)
 
+        before, final = UNITS[last - 1][0], UNITS[last][0]
         for j in reversed(range(2)):
             turn(last - 1, j)
-        weigh(last, slice(0, 1))
-        round_sorted(last, 0, A, True)
-        for j in range(2):
-            gather(12 + j, True)
-        for g in range(GROUPS):
-            weigh(last, slice(1, 2), slice(512 * g, 512 * (g + 1)))
-        turn(last, 0, tag="fit", bufs=4, in_order=True)
-        for g in range(GROUPS):
-            round_sorted(last, A + 512 * g, A + 512 * (g + 1), False)
-        gather(14, True)
-        turn(last, 1, tag="fit", bufs=4, in_order=True)
-        for g in range(GROUPS):
-            quantize_y(10, 2, g)
-        quantize_y(12, 2, 0)
-        gather(15, TAIL_S)
-        quantize_y(12, 2, 1)
-        for g in range(GROUPS):
-            quantize_y(14, 2, g)
-        store_scales(10, 6)
+        weigh(last, side_0)
+        round_sorted(last, 0, A, nc.scalar.copy)
+        gather(before)
+        gather(before + 1)
+        for g in range(HALVES):
+            weigh(last, side_1, slice(HALF * g, HALF * (g + 1)))
+        turn(last, 0, tag="fit", bufs=FIT_BANKS)
+        for g in range(HALVES):
+            round_sorted(last, A + HALF * g, HALF, nc.vector.tensor_copy)
+        gather(final)
+        turn(last, 1, tag="fit", bufs=FIT_BANKS)
+        gather(final + 1)
+        for plane_set in tail_sets:
+            for g in range(HALVES):
+                quantize_y(plane_set, g)
+        store_scales(tail_sets[0][0], TILES - tail_sets[0][0], nc.scalar)

@@ -213,14 +213,17 @@ def tile_radar_azimuth_harmonic_residuals_k5_kernel(
                         op=ALU.subtract,
                     )
 
-        def weigh(k, tiles=slice(None), cols=slice(None)):
+        def weigh(k, start, stop):
             first, count = UNITS[k]
             pair, side = divmod(first, 2)
-            part = y[k][:, tiles, cols]
-            factor = weight[pair][:, side : side + count, :]
-            nc.vector.tensor_tensor(out=part, in0=part, in1=factor[:, tiles, cols], op=ALU.mult)
+            part = y[k][:].rearrange("p j a -> p (j a)")[:, start:stop]
+            factor = weight[pair][:, side : side + count, :].rearrange("p j a -> p (j a)")[:, start:stop]
+            nc.vector.tensor_tensor(out=part, in0=part, in1=factor, op=ALU.mult)
+
+        def store_y(k, tiles=slice(None)):
+            first, count = UNITS[k]
             dst = out_0[P * first : P * (first + count), :].rearrange("(j p) a -> p j a", p=P)
-            nc.sync.dma_start(out=dst[:, tiles, cols], in_=part)
+            nc.sync.dma_start(out=dst[:, tiles, :], in_=y[k][:, tiles, :])
 
         def round_views(k):
             if k not in y_bf:
@@ -280,8 +283,10 @@ def tile_radar_azimuth_harmonic_residuals_k5_kernel(
                 scales=y_sc[:, g, P * first : P * (first + count)],
                 in_=y_words[first][:, g, :],
             )
-            if g == HALVES - 1:
-                dst = out_1.rearrange("g p m t -> p g (m t)")[:, :, PACK * P * first : PACK * P * (first + count)]
+            dst = out_1.rearrange("g p m t -> p g (m t)")[:, :, PACK * P * first : PACK * P * (first + count)]
+            if plane_set == PLANE_SETS[-1]:
+                nc.sync.dma_start(out=dst[:, g, :].bitcast(I32), in_=y_codes[first][:, g, :].bitcast(I32))
+            elif g == HALVES - 1:
                 nc.sync.dma_start(out=dst.bitcast(I32), in_=y_codes[first][:].bitcast(I32))
 
         def store_scales(first, count, queue):
@@ -382,8 +387,10 @@ def tile_radar_azimuth_harmonic_residuals_k5_kernel(
                 project(project_at[k][0], reversed(project_at[k][1]))
             if k >= 2:
                 square(k)
-            weigh(k)
+            weigh(k, 0, plain_columns(k))
             round_plain(k)
+            weigh(k, plain_columns(k), plain_columns(k) + HALF)
+            store_y(k)
             subtract(k + 1)
             if k >= 1 and k + ROW_BUFS - 1 < PAIRS:
                 load_distance(k + ROW_BUFS - 1)
@@ -407,12 +414,14 @@ def tile_radar_azimuth_harmonic_residuals_k5_kernel(
         before, final = UNITS[last - 1][0], UNITS[last][0]
         for j in reversed(range(2)):
             turn(last - 1, j)
-        weigh(last, side_0)
+        weigh(last, 0, A)
+        store_y(last, side_0)
         round_sorted(last, 0, A, nc.scalar.copy)
         gather(before)
         gather(before + 1)
         for g in range(HALVES):
-            weigh(last, side_1, slice(HALF * g, HALF * (g + 1)))
+            weigh(last, A + HALF * g, A + HALF * (g + 1))
+        store_y(last, side_1)
         turn(last, 0, tag="fit", bufs=FIT_BANKS)
         for g in range(HALVES):
             round_sorted(last, A + HALF * g, HALF, nc.vector.tensor_copy)

from contextlib import ExitStack

import concourse.mybir as mybir
from concourse.masks import make_identity

R, A, H = 2048, 1024, 512
FLOPS = 2 * R * A * H * 2

F32 = mybir.dt.float32
BF16 = mybir.dt.bfloat16
I32 = mybir.dt.int32
U32 = mybir.dt.uint32
U8 = mybir.dt.uint8
FP8X4 = mybir.dt.float8_e4m3fn_x4
FP4X4 = mybir.dt.float4_e2m1fn_x4
ACT = mybir.ActivationFunctionType
ALU = mybir.AluOpType

P = 128
PACK = 4
HALF = 512
HALVES = A // HALF
TILES = R // P
PAIRS = TILES // 2

CHUNKS = [(0, 1), (1, 1), (2, 2)] + [(first, 4) for first in range(4, TILES, 4)]
UNITS = [(0, 1), (1, 1)] + [(first, 2) for first in range(2, TILES, 2)]
PLANE_SETS = [(0, 4), (4, 4)] + [(first, 2) for first in range(8, TILES, 2)]
WORD_LOADS = [(0, 4), (4, 4), (8, 8)]
ROW_BUFS = 5
FIT_BANKS = 4


def owner(table, tile):
    return [entry for entry in table if entry[0] <= tile < entry[0] + entry[1]][0]


def unit_of(tile):
    return UNITS.index(owner(UNITS, tile))


def tile_radar_azimuth_harmonic_residuals_k5_kernel(
    tc, vel_words, vel_scales, har_words, har_scales, taper, background, refit, velocity, distance, out_0, out_1, out_2
):
    nc = tc.nc
    with ExitStack() as ctx:
        keep = ctx.enter_context(tc.tile_pool(name="keep", bufs=1))
        flow = ctx.enter_context(tc.tile_pool(name="flow", bufs=2))
        psum = ctx.enter_context(tc.psum_pool(name="psum", bufs=2))
        ctx.enter_context(tc.manual_schedule())

        ident = keep.tile([P, P], F32, name="ident")
        har_raw = keep.tile([P, HALVES, 2 * H], U8, name="har_raw", align_bytes=64)
        har_sc_raw = keep.tile([P, HALVES, H], U8, name="har_sc_raw", align_bytes=64)
        har_codes = keep.tile([P, HALVES, PACK, 2 * P], U8, name="har_codes", align_bytes=64)
        har_sc = keep.tile([P, HALVES, PACK, P], U8, name="har_sc", align_bytes=64)
        vel_sc = keep.tile([P, HALVES, R], U8, name="vel_sc", align_bytes=64)
        taper_bf = keep.tile([P, PACK], BF16, name="taper_bf")
        back_bf = keep.tile([P, PACK], BF16, name="back_bf")
        taper_f = keep.tile([P, PACK], F32, name="taper_f")
        y_sc = keep.tile([P, HALVES, R], U8, name="y_sc", align_bytes=64)

        vel_codes = {}
        vel_rows, dist_rows, weight = {}, {}, {}
        refit_raw, refit_words, refit_mx = {}, {}, {}
        c_bank = {}
        c_slots, c_words, c_mx = {}, {}, {}
        fit = {}
        y, y_bf = {}, {}
        turned = {}
        y_words, y_codes = {}, {}

        def load_scale_rows(plane, rows):
            for q in range(4):
                nc.sync.dma_start(
                    out=plane[32 * q : 32 * q + 4, :, :].bitcast(I32),
                    in_=rows.rearrange("g q n -> q g n")[4 * q : 4 * q + 4, :, :].bitcast(I32),
                )

        def load_words(first, count):
            codes = keep.tile([P, HALVES, 2 * P * count], U8, name="vel_codes%d" % first, align_bytes=64)
            nc.sync.dma_start(
                out=codes[:].bitcast(I32),
                in_=vel_words.rearrange("g p n -> p g n")[:, :, 2 * P * first : 2 * P * (first + count)].bitcast(I32),
            )
            vel_codes[first] = codes

        def load_rows(store, src, label, pair, sides=slice(None)):
            if pair not in store:
                store[pair] = flow.tile([P, 2, A], BF16, name=label, tag=label, bufs=ROW_BUFS)
            rows = src[2 * P * pair : 2 * P * (pair + 1), :].rearrange("(j p) a -> p j a", p=P)
            nc.sync.dma_start(out=store[pair][:, sides, :], in_=rows[:, sides, :])

        def load_distance(pair, sides=slice(None)):
            load_rows(dist_rows, distance, "dist", pair, sides)

        def load_velocity(pair):
            load_rows(vel_rows, velocity, "vel", pair)

        def load_refit(g):
            raw = keep.tile([P, PACK, HALF], BF16, name="refit_raw%d" % g)
            nc.sync.dma_start(out=raw[:], in_=refit[:, HALF * g : HALF * (g + 1)].rearrange("(p t) a -> p t a", t=PACK))
            refit_raw[g] = raw

        def interleave(dst, src):
            nc.vector.tensor_copy(
                out=dst.rearrange("p (c i) t -> p c t i", i=4), in_=src.rearrange("p t (c i) -> p c t i", i=4)
            )

        def quantize_words(words, label):
            width = words.shape[1]
            codes = keep.tile([P, width], U32, name=label + "_codes", align_bytes=64)
            scales = keep.tile([P, width], U8, name=label + "_sc", align_bytes=64)
            nc.vector.quantize_mx(
                out=codes[:].bitcast(FP8X4), scales=scales[:], in_=words[:].rearrange("p c t -> p (c t)")
            )
            return codes, scales

        def interleave_refit(g):
            refit_words[g] = keep.tile([P, HALF, PACK], BF16, name="refit_words%d" % g, align_bytes=64)
            interleave(refit_words[g][:], refit_raw[g][:])

        def quantize_refit(g):
            refit_mx[g] = quantize_words(refit_words[g], "refit%d" % g)

        def slot_columns(chunk, t):
            first, count = chunk
            per_bank = PACK // count
            start = P * count * (t % per_bank)
            return c_bank[first, t // per_bank][:, start : start + P * count]

        def project(chunk, slots, tag="c_bank"):
            first, count = chunk
            per_bank = PACK // count
            load_first = owner(WORD_LOADS, first)[0]
            start = 2 * P * (first - load_first)
            for t in slots:
                if t % per_bank == 0:
                    c_bank[first, t // per_bank] = psum.tile([P, HALF], F32, name="c_bank", tag=tag, bufs=2)
                for g in range(HALVES):
                    nc.tensor.matmul_mx(
                        out=slot_columns(chunk, t),
                        lhsT=har_codes[:, g, t, :].bitcast(FP4X4),
                        lhsT_scale=har_sc[:, g, t, :],
                        rhs=vel_codes[load_first][:, g, start : start + 2 * P * count].bitcast(FP4X4),
                        rhs_scale=vel_sc[:, g, P * first : P * (first + count)],
                        start=(g == 0),
                        stop=(g == HALVES - 1),
                    )

        def apply_taper(chunk, slots):
            first, count = chunk
            for t in slots:
                if t == 0:
                    c_slots[first] = flow.tile([P, PACK, P * count], BF16, name="c_slots", tag="c_slots", bufs=2)
                nc.scalar.activation(
                    out=c_slots[first][:, t, :],
                    in_=slot_columns(chunk, t),
                    func=ACT.Identity,
                    scale=taper_f[:, t : t + 1],
                    bias=back_bf[:, t : t + 1],
                )

        def interleave_c(chunk):
            first, count = chunk
            c_words[first] = flow.tile(
                [P, P * count, PACK], BF16, name="c_words", tag="c_words", bufs=2, align_bytes=64
            )
            interleave(c_words[first][:], c_slots[first][:])

        def quantize_c(chunk):
            c_mx[chunk[0]] = quantize_words(c_words[chunk[0]], "c%d" % chunk[0])

        def refit_rings(k, backwards=False, halves=(1, 0)):
            tiles = range(UNITS[k][0], UNITS[k][0] + UNITS[k][1])
            for j in reversed(tiles) if backwards else tiles:
                first = owner(CHUNKS, j)[0]
                codes, scales = c_mx[first]
                rings = slice(P * (j - first), P * (j - first + 1))
                for g in halves:
                    fit[j, g] = psum.tile([P, HALF], F32, name="fit", tag="fit", bufs=FIT_BANKS)
                    nc.tensor.matmul_mx(
                        out=fit[j, g][:],
                        lhsT=codes[:, rings].bitcast(FP8X4),
                        lhsT_scale=scales[:, rings],
                        rhs=refit_mx[g][0][:].bitcast(FP8X4),
                        rhs_scale=refit_mx[g][1][:],
                        start=True,
                        stop=True,
                    )

        def square(pair, sides=slice(None)):
            if pair not in weight:
                weight[pair] = flow.tile([P, 2, A], F32, name="weight", tag="weight", bufs=3)
            nc.scalar.activation(out=weight[pair][:, sides, :], in_=dist_rows[pair][:, sides, :], func=ACT.Square)

        def gaussian(pair, sides=slice(None)):
            part = weight[pair][:, sides, :]
            nc.scalar.activation(out=part, in_=part, func=ACT.Exp, scale=-1.0)

        def subtract(k, halves=(0, 1)):
            first, count = UNITS[k]
            if k not in y:
                y[k] = flow.tile([P, count, A], F32, name="y", tag="y", bufs=4)
            for j in range(count):
                pair, side = divmod(first + j, 2)
                for g in halves:
                    cols = slice(HALF * g, HALF * (g + 1))
                    nc.vector.tensor_tensor(
                        out=y[k][:, j, cols],
                        in0=vel_rows[pair][:, side, cols],
                        in1=fit[first + j, g][:],
                        op=ALU.subtract,
                    )

        def weigh(k, start, stop):
            first, count = UNITS[k]
            pair, side = divmod(first, 2)
            part = y[k][:].rearrange("p j a -> p (j a)")[:, start:stop]
            factor = weight[pair][:, side : side + count, :].rearrange("p j a -> p (j a)")[:, start:stop]
            nc.vector.tensor_tensor(out=part, in0=part, in1=factor, op=ALU.mult)

        def store_y(k, tiles=slice(None)):
            first, count = UNITS[k]
            dst = out_0[P * first : P * (first + count), :].rearrange("(j p) a -> p j a", p=P)
            nc.sync.dma_start(out=dst[:, tiles, :], in_=y[k][:, tiles, :])

        def round_views(k):
            if k not in y_bf:
                y_bf[k] = flow.tile([P, UNITS[k][1] * A], BF16, name="y_bf", tag="y_bf", bufs=2, align_bytes=64)
            return y_bf[k], y[k][:].rearrange("p j a -> p (j a)")

        def plain_columns(k):
            return A * UNITS[k][1] - HALF if k < len(UNITS) - 1 else 0

        def round_plain(k):
            dst, src = round_views(k)
            cols = slice(0, plain_columns(k))
            nc.gpsimd.tensor_scalar(
                out=dst[:, cols], in0=src[:, cols], scalar1=1.0, scalar2=1.0, op0=ALU.mult, op1=ALU.mult
            )

        def round_sorted(k, start, width, copy):
            dst, src = round_views(k)
            copy(
                out=dst[:, start : start + width].rearrange("p (g u m e) -> p g u m e", u=2, m=P, e=2),
                in_=src[:, start : start + width].rearrange("p (g m u e) -> p g u m e", u=2, m=P, e=2),
            )

        def turn(k, j, tag="turned", bufs=2):
            words = y_bf[k][:].bitcast(F32)
            bank = psum.tile([P, 2 * HALVES, P], F32, name="turned", tag=tag, bufs=bufs)
            for g in range(HALVES):
                start = 2 * P * (HALVES * j + g)
                for u in range(2):
                    if 2 * start < plain_columns(k):
                        src = words[:, start + u : start + 2 * P : 2]
                    else:
                        src = words[:, start + P * u : start + P * (u + 1)]
                    nc.tensor.transpose(bank[:, 2 * g + u, :], src, ident[:])
            turned[UNITS[k][0] + j] = bank

        def gather(j):
            first, count = owner(PLANE_SETS, j)
            if first not in y_words:
                y_words[first] = flow.tile(
                    [P, HALVES, PACK * P * count], BF16, name="y_words", tag="y_words", bufs=4, align_bytes=64
                )
            words = y_words[first][:].bitcast(F32)[:, :, 2 * P * (j - first) : 2 * P * (j - first + 1)]
            nc.scalar.copy(
                out=words.rearrange("p g (r u) -> p g r u", u=2),
                in_=turned[j][:].rearrange("p (g u) r -> p g r u", u=2),
            )

        def quantize_y(plane_set, g):
            first, count = plane_set
            if g == 0:
                y_codes[first] = flow.tile(
                    [P, HALVES, P * count], U32, name="y_codes", tag="y_codes", bufs=3, align_bytes=64
                )
            nc.vector.quantize_mx(
                out=y_codes[first][:, g, :].bitcast(FP8X4),
                scales=y_sc[:, g, P * first : P * (first + count)],
                in_=y_words[first][:, g, :],
            )
            dst = out_1.rearrange("g p m t -> p g (m t)")[:, :, PACK * P * first : PACK * P * (first + count)]
            if plane_set == PLANE_SETS[-1]:
                nc.sync.dma_start(out=dst[:, g, :].bitcast(I32), in_=y_codes[first][:, g, :].bitcast(I32))
            elif g == HALVES - 1:
                nc.sync.dma_start(out=dst.bitcast(I32), in_=y_codes[first][:].bitcast(I32))

        def store_scales(first, count, queue):
            rings = slice(P * first, P * (first + count))
            for q in range(4):
                queue.dma_start(
                    out=out_2.rearrange("g q m -> q g m")[4 * q : 4 * q + 4, :, rings].bitcast(I32),
                    in_=y_sc[32 * q : 32 * q + 4, :, rings].bitcast(I32),
                )

        nc.gpsimd.memset(har_sc_raw[:].rearrange("p g n -> p (g n)").bitcast(I32), 0)
        make_identity(nc, ident[:])
        nc.vector.memset(vel_sc[:].rearrange("p g n -> p (g n)").bitcast(I32), 0)

        side_0, side_1 = slice(0, 1), slice(1, 2)
        nc.sync.dma_start(out=har_raw[:].bitcast(I32), in_=har_words.rearrange("g p n -> p g n").bitcast(I32))
        load_scale_rows(har_sc_raw, har_scales)
        load_distance(0, side_0)
        load_refit(0)
        load_distance(0, side_1)
        load_scale_rows(vel_sc, vel_scales)
        load_words(*WORD_LOADS[0])
        load_refit(1)
        nc.sync.dma_start(out=taper_bf[:], in_=taper.rearrange("(p t) -> p t", t=PACK))
        nc.sync.dma_start(out=back_bf[:], in_=background.rearrange("(p t) -> p t", t=PACK))
        load_words(*WORD_LOADS[1])
        load_velocity(0)
        load_distance(1)
        load_velocity(1)
        load_words(*WORD_LOADS[2])
        for pair in range(2, ROW_BUFS):
            load_distance(pair)
            load_velocity(pair)

        nc.vector.tensor_copy(
            out=har_codes[:].rearrange("p g t (m b) -> p g t m b", b=2),
            in_=har_raw[:].rearrange("p g (m t b) -> p g t m b", t=PACK, b=2),
        )
        nc.vector.tensor_copy(out=har_sc[:], in_=har_sc_raw[:].rearrange("p g (m t) -> p g t m", t=PACK))

        all_slots, low_slots, high_slots = range(PACK), range(2), range(2, PACK)
        project(CHUNKS[0], all_slots)
        project(CHUNKS[1], all_slots)
        project(CHUNKS[2], all_slots, tag="turned")
        square(0, side_0)
        gaussian(0, side_0)
        square(0, side_1)
        nc.scalar.copy(out=taper_f[:], in_=taper_bf[:])
        interleave_refit(0)
        apply_taper(CHUNKS[0], all_slots)
        quantize_refit(0)
        interleave_refit(1)
        interleave_c(CHUNKS[0])
        quantize_c(CHUNKS[0])
        refit_rings(0, halves=(0,))
        quantize_refit(1)
        apply_taper(CHUNKS[1], all_slots)
        refit_rings(0, halves=(1,))
        project(CHUNKS[3], low_slots)
        interleave_c(CHUNKS[1])
        apply_taper(CHUNKS[2], all_slots)
        gaussian(0, side_1)
        subtract(0, halves=(0,))
        quantize_c(CHUNKS[1])
        refit_rings(1)
        interleave_c(CHUNKS[2])
        subtract(0, halves=(1,))
        quantize_c(CHUNKS[2])
        apply_taper(CHUNKS[3], low_slots)
        project(CHUNKS[3], high_slots)
        square(1)
        apply_taper(CHUNKS[3], high_slots)
        gaussian(1)

        last = len(UNITS) - 1
        quantize_c_at = {unit_of(chunk[0]) - 2: chunk for chunk in CHUNKS[3:]}
        project_at = {}
        for chunk in CHUNKS[4:]:
            project_at[unit_of(chunk[0]) - 4] = (chunk, low_slots)
            project_at[unit_of(chunk[0]) - 3] = (chunk, high_slots)
        loop_sets, tail_sets = PLANE_SETS[:-3], PLANE_SETS[-3:]
        quantize_y_at = {}
        for first, count in loop_sets:
            for g in range(HALVES):
                step = unit_of(first + count - 1) + 1 + (g if count == 4 else 0)
                quantize_y_at.setdefault(step, []).append(((first, count), g))

        for k in range(last):
            if k >= 1:
                codes_come_late = k - 1 in quantize_c_at
                if not codes_come_late:
                    refit_rings(k + 1, backwards=k > 1)
                for j in reversed(range(UNITS[k - 1][1])):
                    turn(k - 1, j)
                if codes_come_late:
                    refit_rings(k + 1)
            if k in project_at:
                project(project_at[k][0], reversed(project_at[k][1]))
            if k >= 2:
                square(k)
            weigh(k, 0, plain_columns(k))
            round_plain(k)
            weigh(k, plain_columns(k), plain_columns(k) + HALF)
            store_y(k)
            subtract(k + 1)
            if k >= 1 and k + ROW_BUFS - 1 < PAIRS:
                load_distance(k + ROW_BUFS - 1)
                load_velocity(k + ROW_BUFS - 1)
            if k >= 1:
                for j in range(UNITS[k - 1][1]):
                    gather(UNITS[k - 1][0] + j)
            if k >= 2:
                gaussian(k)
            if k in project_at:
                apply_taper(*project_at[k])
            round_sorted(k, plain_columns(k), HALF, nc.scalar.copy if k == last - 1 else nc.vector.tensor_copy)
            if k in quantize_c_at:
                interleave_c(quantize_c_at[k])
            for plane_set, g in quantize_y_at.get(k, []):
                quantize_y(plane_set, g)
            if k in quantize_c_at:
                quantize_c(quantize_c_at[k])
        store_scales(0, tail_sets[0][0], nc.sync)

        before, final = UNITS[last - 1][0], UNITS[last][0]
        for j in reversed(range(2)):
            turn(last - 1, j)
        weigh(last, 0, A)
        store_y(last, side_0)
        round_sorted(last, 0, A, nc.scalar.copy)
        gather(before)
        gather(before + 1)
        for g in range(HALVES):
            weigh(last, A + HALF * g, A + HALF * (g + 1))
        store_y(last, side_1)
        turn(last, 0, tag="fit", bufs=FIT_BANKS)
        for g in range(HALVES):
            round_sorted(last, A + HALF * g, HALF, nc.vector.tensor_copy)
        gather(final)
        turn(last, 1, tag="fit", bufs=FIT_BANKS)
        gather(final + 1)
        for plane_set in tail_sets:
            for g in range(HALVES):
                quantize_y(plane_set, g)
        store_scales(tail_sets[0][0], TILES - tail_sets[0][0], nc.scalar)
